import numpy as np
import ml_dtypes


def mxq(x, axis, fmt="e4m3"):
    dtype, down = {"e4m3": (ml_dtypes.float8_e4m3fn, 7), "e5m2": (ml_dtypes.float8_e5m2, 14)}[fmt]
    v = np.moveaxis(np.asarray(x, np.float32).astype(ml_dtypes.bfloat16).astype(np.float64), axis, -1)
    blocks = v.reshape(v.shape[:-1] + (-1, 32))
    amax = np.abs(blocks).max(-1, keepdims=True)
    byte = np.maximum(np.where(amax > 0, np.frexp(amax)[1] - 1 + 127, 0) - down, 1)
    scale = np.exp2(byte - 127.0)
    codes = (blocks / scale).astype(np.float32).astype(dtype).astype(np.float64)
    return np.moveaxis((codes * scale).reshape(v.shape), -1, axis)


WIDE = False


def mx_kscale(k):
    if not WIDE:
        return np.ones(k)
    levels = np.array([10, -10, 5, -5, 0])
    if k % 512:
        return np.exp2(np.random.permutation(np.resize(levels, k // 32))).repeat(32)
    a = np.empty((k // 512, 16))
    for p in range(k // 512):
        a[p, :8] = np.random.permutation(np.resize(levels, 8))
        for g in range(8):
            far = levels[np.abs(levels - a[p, g]) >= 10]
            a[p, g + 8] = far[np.random.randint(len(far))]
    return np.exp2(a.ravel()).repeat(32)


def f64(x):
    return np.asarray(x).astype(np.float64)


def striped(idx):
    return np.tile(idx.reshape(-1, 16).T, (8, 1)).astype(np.uint16)


def unstriped(offs):
    return offs[:16].T.reshape(-1).astype(np.int64)


E2M1 = np.array([0.0, 0.5, 1.0, 1.5, 2.0, 3.0, 4.0, 6.0, -0.0, -0.5, -1.0, -1.5, -2.0, -3.0, -4.0, -6.0])


def pack_fp4(w):
    k, n = w.shape
    w = f64(np.asarray(w, np.float32).astype(ml_dtypes.bfloat16)).reshape(k // 32, 32, n)
    amax = np.abs(w).max(1)
    mant, ex = np.frexp(amax / 6.0)
    byte = np.clip(np.where(amax > 0, np.where(mant > 0.5, ex, ex - 1) + 127, 1), 1, 254)
    scaled = (w * np.exp2(127.0 - byte)[:, None, :]).reshape(k, n).astype(np.float32)
    c = np.ascontiguousarray(scaled.reshape(k // 512, 128, 4, n).transpose(0, 1, 3, 2)).astype(ml_dtypes.float4_e2m1fn).view(np.uint8) & 0xF
    words = (c[..., 0::2] | (c[..., 1::2] << 4)).reshape(k // 512, 128, 2 * n)
    return np.ascontiguousarray(words), np.ascontiguousarray(byte.astype(np.uint8).reshape(k // 512, 16, n))


def unpack_fp4(words, scales):
    g, _, n = scales.shape
    words = np.ascontiguousarray(words).reshape(g, 128, n, 2)
    nib = np.empty((g, 128, n, 4), np.uint8)
    nib[..., 0::2] = words & 0xF
    nib[..., 1::2] = words >> 4
    vals = E2M1[nib] * np.repeat(np.exp2(scales.astype(np.float64) - 127.0), 8, axis=1)[..., None]
    return vals.transpose(0, 1, 3, 2).reshape(g * 512, n)


def gelu(v):
    return 0.5 * v * (1.0 + np.tanh(np.sqrt(2.0 / np.pi) * (v + 0.044715 * v**3)))


K, T, S, V, H, N = 1024, 2048, 1024, 512, 512, 256


def setup_inputs():
    n = np.random.standard_normal
    s = mx_kscale(K)[:, None]
    u = mx_kscale(H)
    packed_w2 = pack_fp4(n((H, N)) / np.sqrt(2 * H) / u[:, None])
    packed_w3 = pack_fp4(n((H, N)) / np.sqrt(2 * H) / u[:, None])
    return {
        "xT": (n((K, T)) * s).astype(np.float32),
        "w1": (n((K, H)) / np.sqrt(K) / s * u).astype(np.float32),
        "w2_words": packed_w2[0],
        "w2_scales": packed_w2[1],
        "w3_words": packed_w3[0],
        "w3_scales": packed_w3[1],
        "offs": striped(np.random.permutation(T)[:S]),
    }


def reference(xT, w1, w2_words, w2_scales, w3_words, w3_scales, offs):
    xq = mxq(f64(xT)[:, unstriped(offs)], 0, "e4m3")
    h = gelu(mxq(f64(w1), 0, "e4m3").T @ xq)
    low = 0.5 * (h[:, :V] + h[:, V:2 * V])
    high = 0.5 * (h[:, :V] - h[:, V:2 * V])
    return unpack_fp4(w2_words, w2_scales).T @ mxq(low, 0, "e4m3") + unpack_fp4(w3_words, w3_scales).T @ mxq(high, 0, "e4m3")

@@ -1,0 +1,245 @@
+from contextlib import ExitStack
+
+import concourse.mybir as mybir
+
+K, T, S, V, H, N = 1024, 2048, 1024, 512, 512, 256
+FLOPS = 2 * K * H * S + 2 * 2 * H * N * V
+
+F32 = mybir.dt.float32
+BF16 = mybir.dt.bfloat16
+I32 = mybir.dt.int32
+U32 = mybir.dt.uint32
+U16 = mybir.dt.uint16
+U8 = mybir.dt.uint8
+FP8X4 = mybir.dt.float8_e4m3fn_x4
+FP4X4 = mybir.dt.float4_e2m1fn_x4
+ACT = mybir.ActivationFunctionType
+ALU = mybir.AluOpType
+
+P = 128
+PACK = 4
+K_PASS = P * PACK
+LINE = 4
+CHUNKS = ((1024, 1024), (512, 512, 512, 256, 256))
+HALF = V // 2
+SLICE = 128
+
+
+def tile_picked_haar_gelu_e_kernel(
+    tc, xT, w1, w2_words, w2_scales, w3_words, w3_scales, offs, out
+):
+    nc = tc.nc
+    with ExitStack() as ctx:
+        keep = ctx.enter_context(tc.tile_pool(name="keep", bufs=1))
+        ring = ctx.enter_context(tc.tile_pool(name="ring", bufs=2))
+        psum = ctx.enter_context(tc.psum_pool(name="psum", bufs=1))
+
+        def sbuf(shape, dtype, name, tag=None):
+            return keep.tile(shape, dtype, name=name, tag=tag or name, align_bytes=64)
+
+        def staged(shape, dtype, name):
+            return ring.tile(shape, dtype, name=name, tag="staged", align_bytes=64)
+
+        offsets = keep.tile([P, S // 16], U16, name="offsets")
+
+        probe = sbuf([P, 1], F32, "probe")
+        probe_out = sbuf([P, 1], F32, "probe_out")
+        nc.vector.memset(probe[:], 0.0)
+        nc.scalar.activation(probe_out[:], probe[:], ACT.Gelu_apprx_tanh)
+
+        x_scales = sbuf([P, T], U8, "x_scales")
+        nc.vector.memset(x_scales[:].bitcast(I32), 0)
+        w23_scales = sbuf([P, 2 * N], U8, "w23_scales")
+        nc.vector.memset(w23_scales[:].bitcast(I32), 0)
+
+        def load_rows(src, g, c0, width, name):
+            raw = sbuf([P, PACK, width], F32, name)
+            rows = src[g * K_PASS : (g + 1) * K_PASS, c0 : c0 + width]
+            nc.sync.dma_start(out=raw[:], in_=rows.rearrange("(p j) c -> p j c", j=PACK))
+            return raw
+
+        x_raw = {}
+        w23_words = [sbuf([P, 2 * N], U8, "w23_words%d" % i) for i in range(2)]
+        for g in range(2):
+            c0 = 0
+            for width in CHUNKS[g]:
+                x_raw[g, c0] = load_rows(xT, g, c0, width, "x_raw_%d_%d" % (g, c0))
+                c0 = c0 + width
+            if g == 0:
+                w1_raw0 = load_rows(w1, 0, 0, H, "w1_raw0")
+                nc.sync.dma_start(offsets[:], offs)
+        w1_raw1 = [load_rows(w1, 1, 0, H // 2, "w1_raw1_0")]
+        nc.sync.dma_start(out=w23_words[0][:].bitcast(I32), in_=w2_words[0].bitcast(I32))
+        w1_raw1.append(load_rows(w1, 1, H // 2, H // 2, "w1_raw1_%d" % (H // 2)))
+        nc.sync.dma_start(out=w23_words[1][:].bitcast(I32), in_=w3_words[0].bitcast(I32))
+        for i, (words, scales) in enumerate(((w2_words, w2_scales), (w3_words, w3_scales))):
+            for q in range(4):
+                nc.sync.dma_start(
+                    out=w23_scales[32 * q : 32 * q + 4, N * i : N * (i + 1)].bitcast(I32),
+                    in_=scales[0, 4 * q : 4 * q + 4, :].bitcast(I32),
+                )
+
+        w1_codes = [sbuf([P, H], U32, "w1_codes%d" % g) for g in range(2)]
+        w1_scales = [sbuf([P, H], U8, "w1_scales%d" % g) for g in range(2)]
+        x_codes = [sbuf([P, T], U32, "x_codes%d" % g) for g in range(2)]
+
+        def quantize_x(g):
+            c0 = 0
+            for width in CHUNKS[g]:
+                raw = x_raw[g, c0]
+                step = min(width, 512)
+                for s0 in range(0, width, step):
+                    grouped = staged([P, PACK * step], BF16, "x_bf_%d_%d" % (g, c0 + s0))
+                    split = step * 5 // 8 if step == 512 else step * 3 // 8
+                    dst = grouped[:].rearrange("p (c i t) -> p c t i", i=LINE, t=PACK)
+                    src = raw[:, :, s0 : s0 + step].rearrange("p t (c i) -> p c t i", i=LINE)
+                    a = split // LINE
+                    nc.scalar.activation(dst[:, :a], src[:, :a], ACT.Copy)
+                    nc.vector.tensor_copy(out=dst[:, a:], in_=src[:, a:])
+                    cols = slice(c0 + s0, c0 + s0 + step)
+                    nc.vector.quantize_mx(
+                        out=x_codes[g][:, cols].bitcast(FP8X4), scales=x_scales[4 * g :, cols], in_=grouped[:]
+                    )
+                c0 = c0 + width
+
+        def gather(picked, window, e0, n):
+            nc.vector.tensor_copy(picked, window[:].indirect(offsets[:, e0 // 16 : (e0 + n) // 16]))
+
+        quantize_x(0)
+        codes0 = sbuf([P, S], U32, "codes0")
+        for d in range(2):
+            gather(codes0[:, d * V : (d + 1) * V], x_codes[0], d * V, V)
+        w1_bf0 = sbuf([P, PACK * H], BF16, "w1_bf0")
+        nc.vector.tensor_copy(
+            out=w1_bf0[:].rearrange("p (t m j) -> p m j t", t=PACK, j=PACK),
+            in_=w1_raw0[:].rearrange("p j (m t) -> p m j t", t=PACK),
+        )
+        nc.vector.quantize_mx(out=w1_codes[0][:].bitcast(FP8X4), scales=w1_scales[0][:], in_=w1_bf0[:])
+
+        quantize_x(1)
+
+        def gather_half(half, bytes_tag):
+            codes = staged([P, V], U32, "codes1_%d" % half)
+            planes = sbuf([P, V], U8, "bytes_%d" % half, bytes_tag)
+            for d in range(2):
+                cols = slice(d * HALF, (d + 1) * HALF)
+                gather(codes[:, cols], x_codes[1], d * V + half * HALF, HALF)
+                gather(planes[:, cols], x_scales, d * V + half * HALF, HALF)
+            return codes, planes
+
+        w1_bf1 = staged([P, PACK * H], BF16, "w1_bf1")
+        picked1 = [gather_half(0, None)]
+
+        warm = psum.tile([P, H], F32, name="warm", tag="bank7")
+        for i in range(5):
+            nc.tensor.matmul_mx(
+                out=warm[:],
+                lhsT=w23_words[0][:, : 2 * P].bitcast(FP4X4),
+                lhsT_scale=w1_scales[0][:, :P],
+                rhs=w1_codes[0][:].bitcast(FP8X4),
+                rhs_scale=w1_scales[0][:],
+                start=True,
+                stop=True,
+            )
+
+        for u in range(2):
+            nc.scalar.activation(
+                w1_bf1[:].rearrange("p (t m j) -> p m j t", t=PACK, j=PACK)[:, 64 * u : 64 * (u + 1)],
+                w1_raw1[u][:].rearrange("p j (m t) -> p m j t", t=PACK),
+                ACT.Copy,
+            )
+        nc.vector.quantize_mx(out=w1_codes[1][:].bitcast(FP8X4), scales=w1_scales[1][:], in_=w1_bf1[:])
+
+        picked1.append(gather_half(1, "w1_raw1_%d" % (H // 2)))
+
+        def hidden(s):
+            hs = []
+            for d in range(2):
+                bank = psum.tile([P, PACK, SLICE], F32, name="bank_%d_%d" % (s, d), tag="bank%d" % (2 * s + d))
+                v0 = s * SLICE
+                half, r0 = divmod(v0, HALF)
+                codes1, planes = picked1[half]
+                cols0 = slice(d * V + v0, d * V + v0 + SLICE)
+                cols1 = slice(d * HALF + r0, d * HALF + r0 + SLICE)
+                for t in range(PACK):
+                    m_cols = slice(t * P, (t + 1) * P)
+                    for g in (1, 0):
+                        rhs = codes0[:, cols0] if g == 0 else codes1[:, cols1]
+                        nc.tensor.matmul_mx(
+                            out=bank[:, t, :],
+                            lhsT=w1_codes[g][:, m_cols].bitcast(FP8X4),
+                            lhsT_scale=w1_scales[g][:, m_cols],
+                            rhs=rhs.bitcast(FP8X4),
+                            rhs_scale=planes[4 * g :, cols1],
+                            start=(g == 1),
+                            stop=(g == 0),
+                        )
+                h = sbuf([P, SLICE * PACK], F32, "h_%d_%d" % (s, d))
+                nc.scalar.activation(
+                    h[:].rearrange("p (v t) -> p v t", t=PACK),
+                    bank[:].rearrange("p t v -> p v t"),
+                    ACT.Gelu_apprx_tanh,
+                )
+                hs.append(h)
+            return hs
+
+        BAND = SLICE * PACK
+
+        def band(both, i, hs):
+            nc.vector.tensor_tensor(
+                both[:, i * BAND : (i + 1) * BAND], hs[0][:], hs[1][:], ALU.add if i == 0 else ALU.subtract
+            )
+
+        def band_pass(acc, mt, i, codes, scales):
+            c0 = N * i + P * mt
+            nc.tensor.matmul_mx(
+                out=acc,
+                lhsT=w23_words[i][:, 2 * P * mt : 2 * P * (mt + 1)].bitcast(FP4X4),
+                lhsT_scale=w23_scales[:, c0 : c0 + P],
+                rhs=codes.bitcast(FP8X4),
+                rhs_scale=scales,
+                start=(i == 0),
+                stop=(i == 1),
+            )
+
+        def finish(s, both):
+            codes = sbuf([P, 2 * SLICE], U32, "band_codes_%d" % s)
+            scales = sbuf([P, 2 * SLICE], U8, "band_scales_%d" % s)
+            nc.vector.quantize_mx(out=codes[:].bitcast(FP8X4), scales=scales[:], in_=both[:])
+            acc = psum.tile([P, 2, SLICE], F32, name="acc_%d" % s, tag="bank%d" % (7 - s))
+            for mt in range(2):
+                for i in range(2):
+                    cols = slice(i * SLICE, (i + 1) * SLICE)
+                    band_pass(acc[:, mt, :], mt, i, codes[:, cols], scales[:, cols])
+            result = sbuf([P, 2, SLICE], F32, "result_%d" % s)
+            nc.scalar.activation(result[:], acc[:], ACT.Copy, scale=0.5)
+            nc.sync.dma_start(
+                out=out[:, s * SLICE : (s + 1) * SLICE].rearrange("(mt p) v -> p mt v", p=P), in_=result[:]
+            )
+
+        def finish_last(s, both):
+            accs = [psum.tile([P, SLICE], F32, name="acc_last_%d" % mt, tag="bank%d" % mt) for mt in range(2)]
+            for i in range(2):
+                codes = sbuf([P, SLICE], U32, "last_codes_%d" % i)
+                scales = sbuf([P, SLICE], U8, "last_scales_%d" % i)
+                nc.vector.quantize_mx(
+                    out=codes[:].bitcast(FP8X4), scales=scales[:], in_=both[:, i * BAND : (i + 1) * BAND]
+                )
+                for mt in range(2):
+                    band_pass(accs[mt][:], mt, i, codes[:], scales[:])
+            cols = slice(s * SLICE, (s + 1) * SLICE)
+            results = [sbuf([P, SLICE], F32, "result_last_%d" % mt) for mt in range(2)]
+            nc.vector.tensor_scalar_mul(results[0][:], accs[0][:], 0.5)
+            nc.sync.dma_start(out=out[:P, cols], in_=results[0][:])
+            nc.scalar.activation(results[1][:], accs[1][:], ACT.Copy, scale=0.5)
+            nc.scalar.dma_start(out=out[P:, cols], in_=results[1][:])
+
+        slices = V // SLICE
+        hs = [hidden(s) for s in range(slices)]
+        boths = [sbuf([P, 2 * BAND], BF16, "bands_%d" % s) for s in range(slices)]
+        for s in range(slices):
+            band(boths[s], 0, hs[s])
+            if s > 0:
+                finish(s - 1, boths[s - 1])
+            band(boths[s], 1, hs[s])
+        finish_last(slices - 1, boths[slices - 1])

@@ -20,7 +20,7 @@ P = 128
 PACK = 4
 K_PASS = P * PACK
 LINE = 4
-CHUNKS = ((1024, 1024), (512, 512, 512, 256, 256))
+CHUNKS = ((1024, 1024), (1024, 512, 256, 256))
 HALF = V // 2
 SLICE = 128
 
@@ -35,17 +35,12 @@ def tile_picked_haar_gelu_e_kernel(
         psum = ctx.enter_context(tc.psum_pool(name="psum", bufs=1))
 
         def sbuf(shape, dtype, name, tag=None):
-            return keep.tile(shape, dtype, name=name, tag=tag or name, align_bytes=64)
+            return keep.tile(shape, dtype, name=name, tag=tag or name, align_bytes=256)
 
         def staged(shape, dtype, name):
-            return ring.tile(shape, dtype, name=name, tag="staged", align_bytes=64)
+            return ring.tile(shape, dtype, name=name, tag="staged", align_bytes=256)
 
         offsets = keep.tile([P, S // 16], U16, name="offsets")
-
-        probe = sbuf([P, 1], F32, "probe")
-        probe_out = sbuf([P, 1], F32, "probe_out")
-        nc.vector.memset(probe[:], 0.0)
-        nc.scalar.activation(probe_out[:], probe[:], ACT.Gelu_apprx_tanh)
 
         x_scales = sbuf([P, T], U8, "x_scales")
         nc.vector.memset(x_scales[:].bitcast(I32), 0)
@@ -90,7 +85,7 @@ def tile_picked_haar_gelu_e_kernel(
                 step = min(width, 512)
                 for s0 in range(0, width, step):
                     grouped = staged([P, PACK * step], BF16, "x_bf_%d_%d" % (g, c0 + s0))
-                    split = step * 5 // 8 if step == 512 else step * 3 // 8
+                    split = step * (5 - g) // 8 if step == 512 else step * 3 // 8
                     dst = grouped[:].rearrange("p (c i t) -> p c t i", i=LINE, t=PACK)
                     src = raw[:, :, s0 : s0 + step].rearrange("p t (c i) -> p c t i", i=LINE)
                     a = split // LINE

@@ -19,10 +19,16 @@ ALU = mybir.AluOpType
 P = 128
 PACK = 4
 K_PASS = P * PACK
-LINE = 4
-CHUNKS = ((1024, 1024), (1024, 512, 256, 256))
+PIECES = 2
+LIST_ROWS = 16
+RUN = 4
+SCALE_ROWS = 4
+X_LOADS = ((1024, 512, 512), (512, 512, 512, 256, 256))
+X_STEP = 512
 HALF = V // 2
 SLICE = 128
+BAND = SLICE * PACK
+WARM_UP_PASSES = 5
 
 
 def tile_picked_haar_gelu_e_kernel(
@@ -31,166 +37,157 @@ def tile_picked_haar_gelu_e_kernel(
     nc = tc.nc
     with ExitStack() as ctx:
         keep = ctx.enter_context(tc.tile_pool(name="keep", bufs=1))
-        ring = ctx.enter_context(tc.tile_pool(name="ring", bufs=2))
+        ring = ctx.enter_context(tc.tile_pool(name="ring", bufs=3))
         psum = ctx.enter_context(tc.psum_pool(name="psum", bufs=1))
 
-        def sbuf(shape, dtype, name, tag=None):
+        def held(shape, dtype, name, tag=None):
             return keep.tile(shape, dtype, name=name, tag=tag or name, align_bytes=256)
 
         def staged(shape, dtype, name):
             return ring.tile(shape, dtype, name=name, tag="staged", align_bytes=256)
 
-        offsets = keep.tile([P, S // 16], U16, name="offsets")
+        offsets = keep.tile([P, S // LIST_ROWS], U16, name="offsets")
 
-        x_scales = sbuf([P, T], U8, "x_scales")
+        x_scales = held([P, T], U8, "x_scales")
         nc.vector.memset(x_scales[:].bitcast(I32), 0)
-        w23_scales = sbuf([P, 2 * N], U8, "w23_scales")
+        w23_scales = held([P, 2 * N], U8, "w23_scales")
         nc.vector.memset(w23_scales[:].bitcast(I32), 0)
 
         def load_rows(src, g, c0, width, name):
-            raw = sbuf([P, PACK, width], F32, name)
+            raw = held([P, PACK, width], F32, name)
             rows = src[g * K_PASS : (g + 1) * K_PASS, c0 : c0 + width]
             nc.sync.dma_start(out=raw[:], in_=rows.rearrange("(p j) c -> p j c", j=PACK))
             return raw
 
         x_raw = {}
-        w23_words = [sbuf([P, 2 * N], U8, "w23_words%d" % i) for i in range(2)]
         for g in range(2):
             c0 = 0
-            for width in CHUNKS[g]:
+            for width in X_LOADS[g]:
                 x_raw[g, c0] = load_rows(xT, g, c0, width, "x_raw_%d_%d" % (g, c0))
                 c0 = c0 + width
             if g == 0:
-                w1_raw0 = load_rows(w1, 0, 0, H, "w1_raw0")
                 nc.sync.dma_start(offsets[:], offs)
-        w1_raw1 = [load_rows(w1, 1, 0, H // 2, "w1_raw1_0")]
-        nc.sync.dma_start(out=w23_words[0][:].bitcast(I32), in_=w2_words[0].bitcast(I32))
-        w1_raw1.append(load_rows(w1, 1, H // 2, H // 2, "w1_raw1_%d" % (H // 2)))
-        nc.sync.dma_start(out=w23_words[1][:].bitcast(I32), in_=w3_words[0].bitcast(I32))
-        for i, (words, scales) in enumerate(((w2_words, w2_scales), (w3_words, w3_scales))):
-            for q in range(4):
+        w1_raw = [[load_rows(w1, g, u * H // 2, H // 2, "w1_raw_%d_%d" % (g, u)) for u in range(2)] for g in range(2)]
+        w23_words = []
+        for i, words in enumerate((w2_words, w3_words)):
+            w23_words.append(held([P, 2 * N], U8, "w23_words_%d" % i))
+            nc.sync.dma_start(out=w23_words[i][:].bitcast(I32), in_=words[0].bitcast(I32))
+        for i, scales in enumerate((w2_scales, w3_scales)):
+            for q in range(P // 32):
                 nc.sync.dma_start(
-                    out=w23_scales[32 * q : 32 * q + 4, N * i : N * (i + 1)].bitcast(I32),
-                    in_=scales[0, 4 * q : 4 * q + 4, :].bitcast(I32),
+                    out=w23_scales[32 * q : 32 * q + SCALE_ROWS, N * i : N * (i + 1)].bitcast(I32),
+                    in_=scales[0, SCALE_ROWS * q : SCALE_ROWS * (q + 1), :].bitcast(I32),
                 )
 
-        w1_codes = [sbuf([P, H], U32, "w1_codes%d" % g) for g in range(2)]
-        w1_scales = [sbuf([P, H], U8, "w1_scales%d" % g) for g in range(2)]
-        x_codes = [sbuf([P, T], U32, "x_codes%d" % g) for g in range(2)]
+        x_codes = [held([P, T], U32, "x_codes_%d" % g) for g in range(2)]
 
         def quantize_x(g):
             c0 = 0
-            for width in CHUNKS[g]:
-                raw = x_raw[g, c0]
-                step = min(width, 512)
+            for width in X_LOADS[g]:
+                step = min(width, X_STEP)
                 for s0 in range(0, width, step):
                     grouped = staged([P, PACK * step], BF16, "x_bf_%d_%d" % (g, c0 + s0))
-                    split = step * (5 - g) // 8 if step == 512 else step * 3 // 8
-                    dst = grouped[:].rearrange("p (c i t) -> p c t i", i=LINE, t=PACK)
-                    src = raw[:, :, s0 : s0 + step].rearrange("p t (c i) -> p c t i", i=LINE)
-                    a = split // LINE
-                    nc.scalar.activation(dst[:, :a], src[:, :a], ACT.Copy)
-                    nc.vector.tensor_copy(out=dst[:, a:], in_=src[:, a:])
+                    dst = grouped[:].rearrange("p (c i j) -> p c j i", i=RUN, j=PACK)
+                    src = x_raw[g, c0][:, :, s0 : s0 + step].rearrange("p j (c i) -> p c j i", i=RUN)
+                    runs = step // RUN
+                    on_scalar = runs // 2 if g == 1 and c0 >= T // 2 else runs * 5 // 8
+                    nc.scalar.activation(dst[:, :on_scalar], src[:, :on_scalar], ACT.Copy)
+                    nc.vector.tensor_copy(out=dst[:, on_scalar:], in_=src[:, on_scalar:])
                     cols = slice(c0 + s0, c0 + s0 + step)
                     nc.vector.quantize_mx(
-                        out=x_codes[g][:, cols].bitcast(FP8X4), scales=x_scales[4 * g :, cols], in_=grouped[:]
+                        out=x_codes[g][:, cols].bitcast(FP8X4),
+                        scales=x_scales[SCALE_ROWS * g :, cols],
+                        in_=grouped[:],
                     )
                 c0 = c0 + width
 
-        def gather(picked, window, e0, n):
-            nc.vector.tensor_copy(picked, window[:].indirect(offsets[:, e0 // 16 : (e0 + n) // 16]))
+        def gather(picked, window, entry, count):
+            listed = offsets[:, entry // LIST_ROWS : (entry + count) // LIST_ROWS]
+            nc.vector.tensor_copy(picked, window[:].indirect(listed))
+
+        def gather_half(picked, window, half):
+            for d in range(PIECES):
+                gather(picked[:, d * HALF : (d + 1) * HALF], window, d * V + half * HALF, HALF)
 
         quantize_x(0)
-        codes0 = sbuf([P, S], U32, "codes0")
-        for d in range(2):
+        codes0 = held([P, S], U32, "codes0")
+        for d in range(PIECES):
             gather(codes0[:, d * V : (d + 1) * V], x_codes[0], d * V, V)
-        w1_bf0 = sbuf([P, PACK * H], BF16, "w1_bf0")
-        nc.vector.tensor_copy(
-            out=w1_bf0[:].rearrange("p (t m j) -> p m j t", t=PACK, j=PACK),
-            in_=w1_raw0[:].rearrange("p j (m t) -> p m j t", t=PACK),
-        )
-        nc.vector.quantize_mx(out=w1_codes[0][:].bitcast(FP8X4), scales=w1_scales[0][:], in_=w1_bf0[:])
-
         quantize_x(1)
 
-        def gather_half(half, bytes_tag):
-            codes = staged([P, V], U32, "codes1_%d" % half)
-            planes = sbuf([P, V], U8, "bytes_%d" % half, bytes_tag)
-            for d in range(2):
-                cols = slice(d * HALF, (d + 1) * HALF)
-                gather(codes[:, cols], x_codes[1], d * V + half * HALF, HALF)
-                gather(planes[:, cols], x_scales, d * V + half * HALF, HALF)
-            return codes, planes
+        w1_bf = [held([P, PACK * H], BF16, "w1_bf_0"), staged([P, PACK * H], BF16, "w1_bf_1")]
+        codes1 = [staged([P, V], U32, "codes1_0")]
+        planes = [staged([P, V], U8, "planes_0"), held([P, V], U8, "planes_1", tag="w1_raw_1_0")]
+        codes1.append(staged([P, V], U32, "codes1_1"))
+        gather_half(planes[0], x_scales, 0)
+        gather_half(codes1[0], x_codes[1], 0)
 
-        w1_bf1 = staged([P, PACK * H], BF16, "w1_bf1")
-        picked1 = [gather_half(0, None)]
-
-        warm = psum.tile([P, H], F32, name="warm", tag="bank7")
-        for i in range(5):
+        warm_up = psum.tile([P, V], F32, name="warm_up", tag="bank7")
+        for i in range(WARM_UP_PASSES):
             nc.tensor.matmul_mx(
-                out=warm[:],
-                lhsT=w23_words[0][:, : 2 * P].bitcast(FP4X4),
-                lhsT_scale=w1_scales[0][:, :P],
-                rhs=w1_codes[0][:].bitcast(FP8X4),
-                rhs_scale=w1_scales[0][:],
+                out=warm_up[:],
+                lhsT=codes0[:, :P].bitcast(FP8X4),
+                lhsT_scale=planes[0][:, :P],
+                rhs=codes0[:, :V].bitcast(FP8X4),
+                rhs_scale=planes[0][:],
                 start=True,
                 stop=True,
             )
 
-        for u in range(2):
-            nc.scalar.activation(
-                w1_bf1[:].rearrange("p (t m j) -> p m j t", t=PACK, j=PACK)[:, 64 * u : 64 * (u + 1)],
-                w1_raw1[u][:].rearrange("p j (m t) -> p m j t", t=PACK),
-                ACT.Copy,
-            )
-        nc.vector.quantize_mx(out=w1_codes[1][:].bitcast(FP8X4), scales=w1_scales[1][:], in_=w1_bf1[:])
-
-        picked1.append(gather_half(1, "w1_raw1_%d" % (H // 2)))
-
-        def hidden(s):
-            hs = []
-            for d in range(2):
-                bank = psum.tile([P, PACK, SLICE], F32, name="bank_%d_%d" % (s, d), tag="bank%d" % (2 * s + d))
-                v0 = s * SLICE
-                half, r0 = divmod(v0, HALF)
-                codes1, planes = picked1[half]
-                cols0 = slice(d * V + v0, d * V + v0 + SLICE)
-                cols1 = slice(d * HALF + r0, d * HALF + r0 + SLICE)
-                for t in range(PACK):
-                    m_cols = slice(t * P, (t + 1) * P)
-                    for g in (1, 0):
-                        rhs = codes0[:, cols0] if g == 0 else codes1[:, cols1]
-                        nc.tensor.matmul_mx(
-                            out=bank[:, t, :],
-                            lhsT=w1_codes[g][:, m_cols].bitcast(FP8X4),
-                            lhsT_scale=w1_scales[g][:, m_cols],
-                            rhs=rhs.bitcast(FP8X4),
-                            rhs_scale=planes[4 * g :, cols1],
-                            start=(g == 1),
-                            stop=(g == 0),
-                        )
-                h = sbuf([P, SLICE * PACK], F32, "h_%d_%d" % (s, d))
-                nc.scalar.activation(
-                    h[:].rearrange("p (v t) -> p v t", t=PACK),
-                    bank[:].rearrange("p t v -> p v t"),
-                    ACT.Gelu_apprx_tanh,
+        w1_codes = [held([P, H], U32, "w1_codes_%d" % g) for g in range(2)]
+        w1_scales = [held([P, H], U8, "w1_scales_%d" % g) for g in range(2)]
+        for g in range(2):
+            dealt = w1_bf[g][:].rearrange("p (t m j) -> p m j t", t=PACK, j=PACK)
+            for u in range(2):
+                dst = dealt[:, u * P // 2 : (u + 1) * P // 2]
+                src = w1_raw[g][u][:].rearrange("p j (m t) -> p m j t", t=PACK)
+                if (g, u) == (1, 1):
+                    nc.vector.tensor_copy(out=dst, in_=src)
+                else:
+                    nc.scalar.activation(dst, src, ACT.Copy)
+            for u in range(2):
+                cols = slice(u * H // 2, (u + 1) * H // 2)
+                nc.vector.quantize_mx(
+                    out=w1_codes[g][:, cols].bitcast(FP8X4),
+                    scales=w1_scales[g][:, cols],
+                    in_=w1_bf[g][:, u * PACK * H // 2 : (u + 1) * PACK * H // 2],
                 )
-                hs.append(h)
-            return hs
 
-        BAND = SLICE * PACK
+        gather_half(codes1[1], x_codes[1], 1)
+        gather_half(planes[1], x_scales, 1)
 
-        def band(both, i, hs):
-            nc.vector.tensor_tensor(
-                both[:, i * BAND : (i + 1) * BAND], hs[0][:], hs[1][:], ALU.add if i == 0 else ALU.subtract
+        def hidden(s, d):
+            half, r0 = divmod(s * SLICE, HALF)
+            cols0 = slice(d * V + s * SLICE, d * V + (s + 1) * SLICE)
+            cols1 = slice(d * HALF + r0, d * HALF + r0 + SLICE)
+            bank = psum.tile([P, PACK, SLICE], F32, name="h_bank_%d_%d" % (s, d), tag="bank%d" % (PIECES * s + d))
+            for t in range(PACK):
+                m_cols = slice(t * P, (t + 1) * P)
+                for g, words in ((1, codes1[half][:, cols1]), (0, codes0[:, cols0])):
+                    nc.tensor.matmul_mx(
+                        out=bank[:, t, :],
+                        lhsT=w1_codes[g][:, m_cols].bitcast(FP8X4),
+                        lhsT_scale=w1_scales[g][:, m_cols],
+                        rhs=words.bitcast(FP8X4),
+                        rhs_scale=planes[half][SCALE_ROWS * g :, cols1],
+                        start=(g == 1),
+                        stop=(g == 0),
+                    )
+            h = held([P, BAND], F32, "h_%d_%d" % (s, d))
+            nc.scalar.activation(
+                h[:].rearrange("p (v t) -> p v t", t=PACK), bank[:].rearrange("p t v -> p v t"), ACT.Gelu_apprx_tanh
             )
+            return h
+
+        def band(both, i, pair):
+            op = ALU.add if i == 0 else ALU.subtract
+            nc.vector.tensor_tensor(both[:, i * BAND : (i + 1) * BAND], pair[0][:], pair[1][:], op)
 
         def band_pass(acc, mt, i, codes, scales):
-            c0 = N * i + P * mt
             nc.tensor.matmul_mx(
                 out=acc,
                 lhsT=w23_words[i][:, 2 * P * mt : 2 * P * (mt + 1)].bitcast(FP4X4),
-                lhsT_scale=w23_scales[:, c0 : c0 + P],
+                lhsT_scale=w23_scales[:, N * i + P * mt : N * i + P * (mt + 1)],
                 rhs=codes.bitcast(FP8X4),
                 rhs_scale=scales,
                 start=(i == 0),
@@ -198,43 +195,43 @@ def tile_picked_haar_gelu_e_kernel(
             )
 
         def finish(s, both):
-            codes = sbuf([P, 2 * SLICE], U32, "band_codes_%d" % s)
-            scales = sbuf([P, 2 * SLICE], U8, "band_scales_%d" % s)
+            codes = held([P, 2 * SLICE], U32, "band_codes_%d" % s)
+            scales = held([P, 2 * SLICE], U8, "band_scales_%d" % s)
             nc.vector.quantize_mx(out=codes[:].bitcast(FP8X4), scales=scales[:], in_=both[:])
             acc = psum.tile([P, 2, SLICE], F32, name="acc_%d" % s, tag="bank%d" % (7 - s))
-            for mt in range(2):
+            for mt in range(N // P):
                 for i in range(2):
                     cols = slice(i * SLICE, (i + 1) * SLICE)
                     band_pass(acc[:, mt, :], mt, i, codes[:, cols], scales[:, cols])
-            result = sbuf([P, 2, SLICE], F32, "result_%d" % s)
+            result = held([P, 2, SLICE], F32, "result_%d" % s)
             nc.scalar.activation(result[:], acc[:], ACT.Copy, scale=0.5)
             nc.sync.dma_start(
                 out=out[:, s * SLICE : (s + 1) * SLICE].rearrange("(mt p) v -> p mt v", p=P), in_=result[:]
             )
 
         def finish_last(s, both):
-            accs = [psum.tile([P, SLICE], F32, name="acc_last_%d" % mt, tag="bank%d" % mt) for mt in range(2)]
+            accs = [psum.tile([P, SLICE], F32, name="acc_last_%d" % mt, tag="bank%d" % mt) for mt in range(N // P)]
             for i in range(2):
-                codes = sbuf([P, SLICE], U32, "last_codes_%d" % i)
-                scales = sbuf([P, SLICE], U8, "last_scales_%d" % i)
+                codes = held([P, SLICE], U32, "last_codes_%d" % i)
+                scales = held([P, SLICE], U8, "last_scales_%d" % i)
                 nc.vector.quantize_mx(
                     out=codes[:].bitcast(FP8X4), scales=scales[:], in_=both[:, i * BAND : (i + 1) * BAND]
                 )
-                for mt in range(2):
+                for mt in range(N // P):
                     band_pass(accs[mt][:], mt, i, codes[:], scales[:])
             cols = slice(s * SLICE, (s + 1) * SLICE)
-            results = [sbuf([P, SLICE], F32, "result_last_%d" % mt) for mt in range(2)]
+            results = [held([P, SLICE], F32, "result_last_%d" % mt) for mt in range(N // P)]
             nc.vector.tensor_scalar_mul(results[0][:], accs[0][:], 0.5)
             nc.sync.dma_start(out=out[:P, cols], in_=results[0][:])
             nc.scalar.activation(results[1][:], accs[1][:], ACT.Copy, scale=0.5)
             nc.scalar.dma_start(out=out[P:, cols], in_=results[1][:])
 
         slices = V // SLICE
-        hs = [hidden(s) for s in range(slices)]
-        boths = [sbuf([P, 2 * BAND], BF16, "bands_%d" % s) for s in range(slices)]
+        pairs = [[hidden(s, d) for d in range(PIECES)] for s in range(slices)]
+        bands = [held([P, 2 * BAND], BF16, "bands_%d" % s) for s in range(slices)]
         for s in range(slices):
-            band(boths[s], 0, hs[s])
+            band(bands[s], 0, pairs[s])
             if s > 0:
-                finish(s - 1, boths[s - 1])
-            band(boths[s], 1, hs[s])
-        finish_last(slices - 1, boths[slices - 1])
+                finish(s - 1, bands[s - 1])
+            band(bands[s], 1, pairs[s])
+        finish_last(slices - 1, bands[slices - 1])

@@ -23,12 +23,15 @@ PIECES = 2
 LIST_ROWS = 16
 RUN = 4
 SCALE_ROWS = 4
-X_LOADS = ((1024, 512, 512), (512, 512, 512, 256, 256))
+X_LOADS = ((1024, 1024), (1024, 512, 256, 256))
 X_STEP = 512
+SCALAR_EIGHTHS = (5, 4)
+SCALAR_EIGHTHS_NARROW = 3
 HALF = V // 2
 SLICE = 128
 BAND = SLICE * PACK
-WARM_UP_PASSES = 5
+BANKS = 8
+WARM_UP_PASSES = (2, 3)
 
 
 def tile_picked_haar_gelu_e_kernel(
@@ -37,7 +40,7 @@ def tile_picked_haar_gelu_e_kernel(
     nc = tc.nc
     with ExitStack() as ctx:
         keep = ctx.enter_context(tc.tile_pool(name="keep", bufs=1))
-        ring = ctx.enter_context(tc.tile_pool(name="ring", bufs=3))
+        ring = ctx.enter_context(tc.tile_pool(name="ring", bufs=2))
         psum = ctx.enter_context(tc.psum_pool(name="psum", bufs=1))
 
         def held(shape, dtype, name, tag=None):
@@ -66,10 +69,11 @@ def tile_picked_haar_gelu_e_kernel(
                 x_raw[g, c0] = load_rows(xT, g, c0, width, "x_raw_%d_%d" % (g, c0))
                 c0 = c0 + width
             if g == 0:
+                w1_raw0 = load_rows(w1, 0, 0, H, "w1_raw0")
                 nc.sync.dma_start(offsets[:], offs)
-        w1_raw = [[load_rows(w1, g, u * H // 2, H // 2, "w1_raw_%d_%d" % (g, u)) for u in range(2)] for g in range(2)]
-        w23_words = []
+        w1_raw1, w23_words = [], []
         for i, words in enumerate((w2_words, w3_words)):
+            w1_raw1.append(load_rows(w1, 1, i * H // 2, H // 2, "w1_raw1_%d" % i))
             w23_words.append(held([P, 2 * N], U8, "w23_words_%d" % i))
             nc.sync.dma_start(out=w23_words[i][:].bitcast(I32), in_=words[0].bitcast(I32))
         for i, scales in enumerate((w2_scales, w3_scales)):
@@ -87,10 +91,10 @@ def tile_picked_haar_gelu_e_kernel(
                 step = min(width, X_STEP)
                 for s0 in range(0, width, step):
                     grouped = staged([P, PACK * step], BF16, "x_bf_%d_%d" % (g, c0 + s0))
-                    dst = grouped[:].rearrange("p (c i j) -> p c j i", i=RUN, j=PACK)
-                    src = x_raw[g, c0][:, :, s0 : s0 + step].rearrange("p j (c i) -> p c j i", i=RUN)
-                    runs = step // RUN
-                    on_scalar = runs // 2 if g == 1 and c0 >= T // 2 else runs * 5 // 8
+                    dst = grouped[:].rearrange("p (c r j) -> p c j r", r=RUN, j=PACK)
+                    src = x_raw[g, c0][:, :, s0 : s0 + step].rearrange("p j (c r) -> p c j r", r=RUN)
+                    eighths = SCALAR_EIGHTHS[g] if step == X_STEP else SCALAR_EIGHTHS_NARROW
+                    on_scalar = step // RUN * eighths // 8
                     nc.scalar.activation(dst[:, :on_scalar], src[:, :on_scalar], ACT.Copy)
                     nc.vector.tensor_copy(out=dst[:, on_scalar:], in_=src[:, on_scalar:])
                     cols = slice(c0 + s0, c0 + s0 + step)
@@ -105,61 +109,67 @@ def tile_picked_haar_gelu_e_kernel(
             listed = offsets[:, entry // LIST_ROWS : (entry + count) // LIST_ROWS]
             nc.vector.tensor_copy(picked, window[:].indirect(listed))
 
-        def gather_half(picked, window, half):
-            for d in range(PIECES):
-                gather(picked[:, d * HALF : (d + 1) * HALF], window, d * V + half * HALF, HALF)
+        w1_codes = [held([P, H], U32, "w1_codes_%d" % g) for g in range(2)]
+        w1_scales = [held([P, H], U8, "w1_scales_%d" % g) for g in range(2)]
+
+        def dealt(grouped):
+            return grouped[:].rearrange("p (t m j) -> p m j t", t=PACK, j=PACK)
+
+        def by_channel(raw):
+            return raw[:].rearrange("p j (m t) -> p m j t", t=PACK)
 
         quantize_x(0)
         codes0 = held([P, S], U32, "codes0")
         for d in range(PIECES):
             gather(codes0[:, d * V : (d + 1) * V], x_codes[0], d * V, V)
+
+        w1_bf0 = held([P, PACK * H], BF16, "w1_bf0")
+        nc.vector.tensor_copy(out=dealt(w1_bf0), in_=by_channel(w1_raw0))
+        nc.vector.quantize_mx(out=w1_codes[0][:].bitcast(FP8X4), scales=w1_scales[0][:], in_=w1_bf0[:])
+
         quantize_x(1)
 
-        w1_bf = [held([P, PACK * H], BF16, "w1_bf_0"), staged([P, PACK * H], BF16, "w1_bf_1")]
-        codes1 = [staged([P, V], U32, "codes1_0")]
-        planes = [staged([P, V], U8, "planes_0"), held([P, V], U8, "planes_1", tag="w1_raw_1_0")]
-        codes1.append(staged([P, V], U32, "codes1_1"))
-        gather_half(planes[0], x_scales, 0)
-        gather_half(codes1[0], x_codes[1], 0)
+        w1_bf1 = staged([P, PACK * H], BF16, "w1_bf1")
+        codes1 = [staged([P, V], U32, "codes1_%d" % half) for half in range(2)]
+        planes = [held([P, V], U8, "planes_0"), held([P, V], U8, "planes_1", tag="w1_raw1_1")]
 
-        warm_up = psum.tile([P, V], F32, name="warm_up", tag="bank7")
-        for i in range(WARM_UP_PASSES):
-            nc.tensor.matmul_mx(
-                out=warm_up[:],
-                lhsT=codes0[:, :P].bitcast(FP8X4),
-                lhsT_scale=planes[0][:, :P],
-                rhs=codes0[:, :V].bitcast(FP8X4),
-                rhs_scale=planes[0][:],
-                start=True,
-                stop=True,
-            )
+        def gather_round(half):
+            for d in range(PIECES):
+                cols = slice(d * HALF, (d + 1) * HALF)
+                gather(codes1[half][:, cols], x_codes[1], d * V + half * HALF, HALF)
+                gather(planes[half][:, cols], x_scales, d * V + half * HALF, HALF)
 
-        w1_codes = [held([P, H], U32, "w1_codes_%d" % g) for g in range(2)]
-        w1_scales = [held([P, H], U8, "w1_scales_%d" % g) for g in range(2)]
-        for g in range(2):
-            dealt = w1_bf[g][:].rearrange("p (t m j) -> p m j t", t=PACK, j=PACK)
-            for u in range(2):
-                dst = dealt[:, u * P // 2 : (u + 1) * P // 2]
-                src = w1_raw[g][u][:].rearrange("p j (m t) -> p m j t", t=PACK)
-                if (g, u) == (1, 1):
-                    nc.vector.tensor_copy(out=dst, in_=src)
-                else:
-                    nc.scalar.activation(dst, src, ACT.Copy)
-            for u in range(2):
-                cols = slice(u * H // 2, (u + 1) * H // 2)
-                nc.vector.quantize_mx(
-                    out=w1_codes[g][:, cols].bitcast(FP8X4),
-                    scales=w1_scales[g][:, cols],
-                    in_=w1_bf[g][:, u * PACK * H // 2 : (u + 1) * PACK * H // 2],
+        gather_round(0)
+
+        warm_up = psum.tile([P, H], F32, name="warm_up", tag="bank%d" % (BANKS - 1))
+        for i, passes in enumerate(WARM_UP_PASSES):
+            for repeat in range(passes):
+                nc.tensor.matmul_mx(
+                    out=warm_up[:],
+                    lhsT=w23_words[i][:, : 2 * P].bitcast(FP4X4),
+                    lhsT_scale=w1_scales[0][:, :P],
+                    rhs=w1_codes[0][:].bitcast(FP8X4),
+                    rhs_scale=w1_scales[0][:],
+                    start=True,
+                    stop=True,
                 )
 
-        gather_half(codes1[1], x_codes[1], 1)
-        gather_half(planes[1], x_scales, 1)
+        for u in range(2):
+            nc.scalar.activation(dealt(w1_bf1)[:, u * P // 2 : (u + 1) * P // 2], by_channel(w1_raw1[u]), ACT.Copy)
+        for u in range(2):
+            cols = slice(u * H // 2, (u + 1) * H // 2)
+            nc.vector.quantize_mx(
+                out=w1_codes[1][:, cols].bitcast(FP8X4),
+                scales=w1_scales[1][:, cols],
+                in_=w1_bf1[:, u * PACK * H // 2 : (u + 1) * PACK * H // 2],
+            )
+
+        gather_round(1)
 
         def hidden(s, d):
-            half, r0 = divmod(s * SLICE, HALF)
+            half, place = divmod(s * SLICE, HALF)
             cols0 = slice(d * V + s * SLICE, d * V + (s + 1) * SLICE)
-            cols1 = slice(d * HALF + r0, d * HALF + r0 + SLICE)
+            cols1 = slice(d * HALF + place, d * HALF + place + SLICE)
             bank = psum.tile([P, PACK, SLICE], F32, name="h_bank_%d_%d" % (s, d), tag="bank%d" % (PIECES * s + d))
             for t in range(PACK):
                 m_cols = slice(t * P, (t + 1) * P)
@@ -198,7 +208,7 @@ def tile_picked_haar_gelu_e_kernel(
             codes = held([P, 2 * SLICE], U32, "band_codes_%d" % s)
             scales = held([P, 2 * SLICE], U8, "band_scales_%d" % s)
             nc.vector.quantize_mx(out=codes[:].bitcast(FP8X4), scales=scales[:], in_=both[:])
-            acc = psum.tile([P, 2, SLICE], F32, name="acc_%d" % s, tag="bank%d" % (7 - s))
+            acc = psum.tile([P, 2, SLICE], F32, name="acc_%d" % s, tag="bank%d" % (BANKS - 1 - s))
             for mt in range(N // P):
                 for i in range(2):
                     cols = slice(i * SLICE, (i + 1) * SLICE)

@@ -21,16 +21,13 @@ PACK = 4
 K_PASS = P * PACK
 PIECES = 2
 LIST_ROWS = 16
-RUN = 4
 SCALE_ROWS = 4
-X_LOADS = ((1024, 1024), (1024, 512, 256, 256))
-X_STEP = 512
-SCALAR_EIGHTHS = (5, 4)
-SCALAR_EIGHTHS_NARROW = 3
-HALF = V // 2
+WHOLE_ON_SCALAR = 672
+LAST_LOADS = ((1024, 1024), (512, 0), (512, 128))
+GROUP = 64
+BANKS = 8
 SLICE = 128
 BAND = SLICE * PACK
-BANKS = 8
 WARM_UP_PASSES = (2, 3)
 
 
@@ -40,40 +37,45 @@ def tile_picked_haar_gelu_e_kernel(
     nc = tc.nc
     with ExitStack() as ctx:
         keep = ctx.enter_context(tc.tile_pool(name="keep", bufs=1))
-        ring = ctx.enter_context(tc.tile_pool(name="ring", bufs=2))
         psum = ctx.enter_context(tc.psum_pool(name="psum", bufs=1))
 
         def held(shape, dtype, name, tag=None):
             return keep.tile(shape, dtype, name=name, tag=tag or name, align_bytes=256)
 
-        def staged(shape, dtype, name):
-            return ring.tile(shape, dtype, name=name, tag="staged", align_bytes=256)
-
         offsets = keep.tile([P, S // LIST_ROWS], U16, name="offsets")
 
-        x_scales = held([P, T], U8, "x_scales")
-        nc.vector.memset(x_scales[:].bitcast(I32), 0)
         w23_scales = held([P, 2 * N], U8, "w23_scales")
         nc.vector.memset(w23_scales[:].bitcast(I32), 0)
+        table_warm = held([P, 2], F32, "table_warm")
+        nc.vector.memset(table_warm[:, :1], 0.0)
+        nc.scalar.activation(table_warm[:, 1:], table_warm[:, :1], ACT.Gelu_apprx_tanh)
 
-        def load_rows(src, g, c0, width, name):
-            raw = held([P, PACK, width], F32, name)
-            rows = src[g * K_PASS : (g + 1) * K_PASS, c0 : c0 + width]
-            nc.sync.dma_start(out=raw[:], in_=rows.rearrange("(p j) c -> p j c", j=PACK))
+        def load_rows(src, g, j0, rows, c0, width, name):
+            raw = held([P, rows, width], F32, name)
+            view = src[g * K_PASS : (g + 1) * K_PASS, :].rearrange("(p j) c -> p j c", j=PACK)
+            nc.sync.dma_start(out=raw[:], in_=view[:, j0 : j0 + rows, c0 : c0 + width])
             return raw
 
         x_raw = {}
-        for g in range(2):
-            c0 = 0
-            for width in X_LOADS[g]:
-                x_raw[g, c0] = load_rows(xT, g, c0, width, "x_raw_%d_%d" % (g, c0))
-                c0 = c0 + width
-            if g == 0:
-                w1_raw0 = load_rows(w1, 0, 0, H, "w1_raw0")
-                nc.sync.dma_start(offsets[:], offs)
+        x_raw[0, 0] = [(load_rows(xT, 0, 0, 2, 0, T, "x_raw_00"), 0, T, WHOLE_ON_SCALAR)]
+        nc.sync.dma_start(offsets[:], offs)
+        x_raw[0, 1] = [
+            (load_rows(xT, 0, 2, 2, 0, T // 2, "x_raw_01_0"), 0, T // 2, T // 2),
+            (load_rows(xT, 0, 2, 2, T // 2, T // 2, "x_raw_01_1"), T // 2, T // 2, 320),
+        ]
+        w1_raw0 = load_rows(w1, 0, 0, PACK, 0, H, "w1_raw0")
+        x_raw[1, 0] = [
+            (load_rows(xT, 1, 0, 2, 0, T // 2, "x_raw_10_0"), 0, T // 2, T // 2),
+            (load_rows(xT, 1, 0, 2, T // 2, T // 2, "x_raw_10_1"), T // 2, T // 2, 320),
+        ]
+        x_raw[1, 1] = []
+        c0 = 0
+        for width, on_scalar in LAST_LOADS:
+            x_raw[1, 1].append((load_rows(xT, 1, 2, 2, c0, width, "x_raw_11_%d" % c0), c0, width, on_scalar))
+            c0 = c0 + width
         w1_raw1, w23_words = [], []
         for i, words in enumerate((w2_words, w3_words)):
-            w1_raw1.append(load_rows(w1, 1, i * H // 2, H // 2, "w1_raw1_%d" % i))
+            w1_raw1.append(load_rows(w1, 1, 0, PACK, i * H // 2, H // 2, "w1_raw1_%d" % i))
             w23_words.append(held([P, 2 * N], U8, "w23_words_%d" % i))
             nc.sync.dma_start(out=w23_words[i][:].bitcast(I32), in_=words[0].bitcast(I32))
         for i, scales in enumerate((w2_scales, w3_scales)):
@@ -83,31 +85,32 @@ def tile_picked_haar_gelu_e_kernel(
                     in_=scales[0, SCALE_ROWS * q : SCALE_ROWS * (q + 1), :].bitcast(I32),
                 )
 
-        x_codes = [held([P, T], U32, "x_codes_%d" % g) for g in range(2)]
+        picked = [held([P, 2 * S], U32, "picked_%d" % g) for g in range(2)]
 
-        def quantize_x(g):
-            c0 = 0
-            for width in X_LOADS[g]:
-                step = min(width, X_STEP)
-                for s0 in range(0, width, step):
-                    grouped = staged([P, PACK * step], BF16, "x_bf_%d_%d" % (g, c0 + s0))
-                    dst = grouped[:].rearrange("p (c r j) -> p c j r", r=RUN, j=PACK)
-                    src = x_raw[g, c0][:, :, s0 : s0 + step].rearrange("p j (c r) -> p c j r", r=RUN)
-                    eighths = SCALAR_EIGHTHS[g] if step == X_STEP else SCALAR_EIGHTHS_NARROW
-                    on_scalar = step // RUN * eighths // 8
-                    nc.scalar.activation(dst[:, :on_scalar], src[:, :on_scalar], ACT.Copy)
-                    nc.vector.tensor_copy(out=dst[:, on_scalar:], in_=src[:, on_scalar:])
-                    cols = slice(c0 + s0, c0 + s0 + step)
-                    nc.vector.quantize_mx(
-                        out=x_codes[g][:, cols].bitcast(FP8X4),
-                        scales=x_scales[SCALE_ROWS * g :, cols],
-                        in_=grouped[:],
-                    )
-                c0 = c0 + width
+        def pick(g, u):
+            pairs = held([P, 2 * T], BF16, "x_pairs_%d%d" % (g, u))
+            dst = pairs[:].rearrange("p (c j) -> p c j", j=2)
+            for raw, c0, width, on_scalar in x_raw[g, u]:
+                src = raw[:].rearrange("p j c -> p c j")
+                if on_scalar > 0:
+                    nc.scalar.activation(dst[:, c0 : c0 + on_scalar], src[:, :on_scalar], ACT.Copy)
+                if on_scalar < width:
+                    nc.vector.tensor_copy(out=dst[:, c0 + on_scalar : c0 + width], in_=src[:, on_scalar:])
+            nc.vector.tensor_copy(picked[g][:, u * S : (u + 1) * S], pairs[:].bitcast(U32).indirect(offsets[:]))
 
-        def gather(picked, window, entry, count):
-            listed = offsets[:, entry // LIST_ROWS : (entry + count) // LIST_ROWS]
-            nc.vector.tensor_copy(picked, window[:].indirect(listed))
+        x_mx = {}
+
+        def weave_views(g, half, woven, dtype):
+            src = picked[g][:].bitcast(dtype).rearrange("p (u d b c) -> p b d c u", u=2, d=PIECES, c=GROUP)
+            dst = woven[:].bitcast(dtype).rearrange("p (b d c u) -> p b d c u", u=2, d=PIECES, c=GROUP)
+            return dst, src[:, half * BANKS // 2 : (half + 1) * BANKS // 2]
+
+        def quantize_x(g, b0, banks, woven, name, tag=None):
+            codes = held([P, banks * P], U32, name, tag=tag)
+            scales = held([P, banks * P], U8, name + "_scales")
+            nc.vector.quantize_mx(out=codes[:].bitcast(FP8X4), scales=scales[:], in_=woven)
+            for b in range(banks):
+                x_mx[g, b0 + b] = (codes[:, b * P : (b + 1) * P], scales[:, b * P : (b + 1) * P])
 
         w1_codes = [held([P, H], U32, "w1_codes_%d" % g) for g in range(2)]
         w1_scales = [held([P, H], U8, "w1_scales_%d" % g) for g in range(2)]
@@ -118,28 +121,26 @@ def tile_picked_haar_gelu_e_kernel(
         def by_channel(raw):
             return raw[:].rearrange("p j (m t) -> p m j t", t=PACK)
 
-        quantize_x(0)
-        codes0 = held([P, S], U32, "codes0")
-        for d in range(PIECES):
-            gather(codes0[:, d * V : (d + 1) * V], x_codes[0], d * V, V)
-
+        pick(0, 0)
+        pick(0, 1)
         w1_bf0 = held([P, PACK * H], BF16, "w1_bf0")
-        nc.vector.tensor_copy(out=dealt(w1_bf0), in_=by_channel(w1_raw0))
+        nc.scalar.activation(dealt(w1_bf0), by_channel(w1_raw0), ACT.Copy)
+        woven0 = [held([P, PACK * S // 2], BF16, "woven_00"), held([P, PACK * S // 2], BF16, "woven_01")]
+        dst, src = weave_views(0, 0, woven0[0], I32)
+        nc.vector.tensor_copy(out=dst, in_=src)
+        dst, src = weave_views(0, 1, woven0[1], I32)
+        nc.vector.tensor_copy(out=dst, in_=src)
+        quantize_x(0, 0, 4, woven0[0][:], "x_codes_00")
+        quantize_x(0, 4, 4, woven0[1][:], "x_codes_04")
         nc.vector.quantize_mx(out=w1_codes[0][:].bitcast(FP8X4), scales=w1_scales[0][:], in_=w1_bf0[:])
 
-        quantize_x(1)
-
-        w1_bf1 = staged([P, PACK * H], BF16, "w1_bf1")
-        codes1 = [staged([P, V], U32, "codes1_%d" % half) for half in range(2)]
-        planes = [held([P, V], U8, "planes_0"), held([P, V], U8, "planes_1", tag="w1_raw1_1")]
-
-        def gather_round(half):
-            for d in range(PIECES):
-                cols = slice(d * HALF, (d + 1) * HALF)
-                gather(codes1[half][:, cols], x_codes[1], d * V + half * HALF, HALF)
-                gather(planes[half][:, cols], x_scales, d * V + half * HALF, HALF)
-
-        gather_round(0)
+        pick(1, 0)
+        pick(1, 1)
+        woven10 = held([P, PACK * S // 2], BF16, "woven_10")
+        dst, src = weave_views(1, 0, woven10, I32)
+        nc.vector.tensor_copy(out=dst[:, :2], in_=src[:, :2])
+        nc.vector.tensor_copy(out=dst[:, 2:], in_=src[:, 2:])
+        quantize_x(1, 0, 2, woven10[:, : PACK * 2 * P], "x_codes_10")
 
         warm_up = psum.tile([P, H], F32, name="warm_up", tag="bank%d" % (BANKS - 1))
         for i, passes in enumerate(WARM_UP_PASSES):
@@ -154,6 +155,7 @@ def tile_picked_haar_gelu_e_kernel(
                     stop=True,
                 )
 
+        w1_bf1 = held([P, PACK * H], BF16, "w1_bf1")
         for u in range(2):
             nc.scalar.activation(dealt(w1_bf1)[:, u * P // 2 : (u + 1) * P // 2], by_channel(w1_raw1[u]), ACT.Copy)
         for u in range(2):
@@ -164,34 +166,38 @@ def tile_picked_haar_gelu_e_kernel(
                 in_=w1_bf1[:, u * PACK * H // 2 : (u + 1) * PACK * H // 2],
             )
 
-        gather_round(1)
+        quantize_x(1, 2, 2, woven10[:, PACK * 2 * P :], "x_codes_12", tag="w1_bf1")
+        woven11 = held([P, PACK * S // 2], BF16, "woven_11", tag="w1_raw1_1")
+        dst, src = weave_views(1, 1, woven11, U32)
+        nc.scalar.copy(dst, src)
+        quantize_x(1, 4, 4, woven11[:], "x_codes_14")
 
-        def hidden(s, d):
-            half, place = divmod(s * SLICE, HALF)
-            cols0 = slice(d * V + s * SLICE, d * V + (s + 1) * SLICE)
-            cols1 = slice(d * HALF + place, d * HALF + place + SLICE)
-            bank = psum.tile([P, PACK, SLICE], F32, name="h_bank_%d_%d" % (s, d), tag="bank%d" % (PIECES * s + d))
+        h = [held([P, 2, PIECES, BAND // 2], F32, "h_%d" % s) for s in range(V // SLICE)]
+
+        def hidden(b):
+            bank = psum.tile([P, PACK, P], F32, name="h_bank_%d" % b, tag="bank%d" % b)
             for t in range(PACK):
                 m_cols = slice(t * P, (t + 1) * P)
-                for g, words in ((1, codes1[half][:, cols1]), (0, codes0[:, cols0])):
+                for g in range(2):
                     nc.tensor.matmul_mx(
                         out=bank[:, t, :],
                         lhsT=w1_codes[g][:, m_cols].bitcast(FP8X4),
                         lhsT_scale=w1_scales[g][:, m_cols],
-                        rhs=words.bitcast(FP8X4),
-                        rhs_scale=planes[half][SCALE_ROWS * g :, cols1],
-                        start=(g == 1),
-                        stop=(g == 0),
+                        rhs=x_mx[g, b][0].bitcast(FP8X4),
+                        rhs_scale=x_mx[g, b][1],
+                        start=(g == 0),
+                        stop=(g == 1),
                     )
-            h = held([P, BAND], F32, "h_%d_%d" % (s, d))
             nc.scalar.activation(
-                h[:].rearrange("p (v t) -> p v t", t=PACK), bank[:].rearrange("p t v -> p v t"), ACT.Gelu_apprx_tanh
+                h[b // 2][:, b % 2].rearrange("p d (v t) -> p (d v) t", t=PACK),
+                bank[:].rearrange("p t v -> p v t"),
+                ACT.Gelu_apprx_tanh,
             )
-            return h
 
-        def band(both, i, pair):
+        def band(s, i, b0, b1):
             op = ALU.add if i == 0 else ALU.subtract
-            nc.vector.tensor_tensor(both[:, i * BAND : (i + 1) * BAND], pair[0][:], pair[1][:], op)
+            dst = bands[s][:, i * BAND : (i + 1) * BAND].rearrange("p (b x) -> p b x", b=2)
+            nc.vector.tensor_tensor(dst[:, b0:b1], h[s][:, b0:b1, 0], h[s][:, b0:b1, 1], op)
 
         def band_pass(acc, mt, i, codes, scales):
             nc.tensor.matmul_mx(
@@ -208,7 +214,7 @@ def tile_picked_haar_gelu_e_kernel(
             codes = held([P, 2 * SLICE], U32, "band_codes_%d" % s)
             scales = held([P, 2 * SLICE], U8, "band_scales_%d" % s)
             nc.vector.quantize_mx(out=codes[:].bitcast(FP8X4), scales=scales[:], in_=both[:])
-            acc = psum.tile([P, 2, SLICE], F32, name="acc_%d" % s, tag="bank%d" % (BANKS - 1 - s))
+            acc = psum.tile([P, 2, SLICE], F32, name="acc_%d" % s, tag="bank%d" % (5 + s))
             for mt in range(N // P):
                 for i in range(2):
                     cols = slice(i * SLICE, (i + 1) * SLICE)
@@ -237,11 +243,14 @@ def tile_picked_haar_gelu_e_kernel(
             nc.scalar.dma_start(out=out[P:, cols], in_=results[1][:])
 
         slices = V // SLICE
-        pairs = [[hidden(s, d) for d in range(PIECES)] for s in range(slices)]
+        for b in range(BANKS):
+            hidden(b)
         bands = [held([P, 2 * BAND], BF16, "bands_%d" % s) for s in range(slices)]
-        for s in range(slices):
-            band(bands[s], 0, pairs[s])
-            if s > 0:
-                finish(s - 1, bands[s - 1])
-            band(bands[s], 1, pairs[s])
+        for b in range(2):
+            for i in range(2):
+                band(0, i, b, b + 1)
+        for s in range(1, slices):
+            band(s, 0, 0, 2)
+            finish(s - 1, bands[s - 1])
+            band(s, 1, 0, 2)
         finish_last(slices - 1, bands[slices - 1])

@@ -24,6 +24,7 @@ LIST_ROWS = 16
 SCALE_ROWS = 4
 WHOLE_ON_SCALAR = 672
 LAST_LOADS = ((1024, 1024), (512, 0), (512, 128))
+RUN = 4
 GROUP = 64
 BANKS = 8
 SLICE = 128
@@ -89,21 +90,23 @@ def tile_picked_haar_gelu_e_kernel(
 
         def pick(g, u):
             pairs = held([P, 2 * T], BF16, "x_pairs_%d%d" % (g, u))
-            dst = pairs[:].rearrange("p (c j) -> p c j", j=2)
+            dst = pairs[:].rearrange("p (c r j) -> p c j r", r=RUN, j=2)
             for raw, c0, width, on_scalar in x_raw[g, u]:
-                src = raw[:].rearrange("p j c -> p c j")
-                if on_scalar > 0:
-                    nc.scalar.activation(dst[:, c0 : c0 + on_scalar], src[:, :on_scalar], ACT.Copy)
-                if on_scalar < width:
-                    nc.vector.tensor_copy(out=dst[:, c0 + on_scalar : c0 + width], in_=src[:, on_scalar:])
-            nc.vector.tensor_copy(picked[g][:, u * S : (u + 1) * S], pairs[:].bitcast(U32).indirect(offsets[:]))
+                src = raw[:].rearrange("p j (c r) -> p c j r", r=RUN)
+                a, b, c = c0 // RUN, on_scalar // RUN, width // RUN
+                if b > 0:
+                    nc.scalar.activation(dst[:, a : a + b], src[:, :b], ACT.Copy)
+                if b < c:
+                    nc.vector.tensor_copy(out=dst[:, a + b : a + c], in_=src[:, b:])
+            by_bank = picked[g][:, u * S : (u + 1) * S].rearrange("p (b d c) -> p d b c", d=PIECES, c=GROUP)
+            nc.vector.tensor_copy(by_bank, pairs[:].bitcast(U32).indirect(offsets[:]))
 
         x_mx = {}
 
         def weave_views(g, half, woven, dtype):
-            src = picked[g][:].bitcast(dtype).rearrange("p (u d b c) -> p b d c u", u=2, d=PIECES, c=GROUP)
-            dst = woven[:].bitcast(dtype).rearrange("p (b d c u) -> p b d c u", u=2, d=PIECES, c=GROUP)
-            return dst, src[:, half * BANKS // 2 : (half + 1) * BANKS // 2]
+            src = picked[g][:].bitcast(dtype).rearrange("p (u c r) -> p c u r", u=2, r=2)
+            dst = woven[:].bitcast(dtype).rearrange("p (c r u) -> p c u r", u=2, r=2)
+            return dst, src[:, half * S // 4 : (half + 1) * S // 4]
 
         def quantize_x(g, b0, banks, woven, name, tag=None):
             codes = held([P, banks * P], U32, name, tag=tag)
@@ -138,8 +141,8 @@ def tile_picked_haar_gelu_e_kernel(
         pick(1, 1)
         woven10 = held([P, PACK * S // 2], BF16, "woven_10")
         dst, src = weave_views(1, 0, woven10, I32)
-        nc.vector.tensor_copy(out=dst[:, :2], in_=src[:, :2])
-        nc.vector.tensor_copy(out=dst[:, 2:], in_=src[:, 2:])
+        nc.vector.tensor_copy(out=dst[:, :P], in_=src[:, :P])
+        nc.vector.tensor_copy(out=dst[:, P:], in_=src[:, P:])
         quantize_x(1, 0, 2, woven10[:, : PACK * 2 * P], "x_codes_10")
 
         warm_up = psum.tile([P, H], F32, name="warm_up", tag="bank%d" % (BANKS - 1))

@@ -22,14 +22,20 @@ K_PASS = P * PACK
 PIECES = 2
 LIST_ROWS = 16
 SCALE_ROWS = 4
-WHOLE_ON_SCALAR = 672
-LAST_LOADS = ((1024, 1024), (512, 0), (512, 128))
 RUN = 4
 GROUP = 64
 BANKS = 8
 SLICE = 128
 BAND = SLICE * PACK
-WARM_UP_PASSES = (2, 3)
+X_LOADS = (
+    ((2048, 672),),
+    ((1024, 1024), (1024, 320)),
+    ((1024, 1024), (1024, 320)),
+    ((1024, 1024), (512, 0), (512, 128)),
+)
+W1_LOADS = (192, 192, 128)
+VECTOR_BANKS = 2
+WARM_UP_PASSES = 5
 
 
 def tile_picked_haar_gelu_e_kernel(
@@ -38,47 +44,54 @@ def tile_picked_haar_gelu_e_kernel(
     nc = tc.nc
     with ExitStack() as ctx:
         keep = ctx.enter_context(tc.tile_pool(name="keep", bufs=1))
+        shared = ctx.enter_context(tc.tile_pool(name="shared", bufs=1))
         psum = ctx.enter_context(tc.psum_pool(name="psum", bufs=1))
 
-        def held(shape, dtype, name, tag=None):
-            return keep.tile(shape, dtype, name=name, tag=tag or name, align_bytes=256)
+        def held(shape, dtype, name):
+            return keep.tile(shape, dtype, name=name, align_bytes=256)
+
+        def placed(shape, dtype, name, offset):
+            return shared.tile(shape, dtype, name=name, offset=offset, align_bytes=256)
 
         offsets = keep.tile([P, S // LIST_ROWS], U16, name="offsets")
 
         w23_scales = held([P, 2 * N], U8, "w23_scales")
         nc.vector.memset(w23_scales[:].bitcast(I32), 0)
+
         table_warm = held([P, 2], F32, "table_warm")
         nc.vector.memset(table_warm[:, :1], 0.0)
         nc.scalar.activation(table_warm[:, 1:], table_warm[:, :1], ACT.Gelu_apprx_tanh)
 
-        def load_rows(src, g, j0, rows, c0, width, name):
-            raw = held([P, rows, width], F32, name)
-            view = src[g * K_PASS : (g + 1) * K_PASS, :].rearrange("(p j) c -> p j c", j=PACK)
-            nc.sync.dma_start(out=raw[:], in_=view[:, j0 : j0 + rows, c0 : c0 + width])
+        def load_rows(raw, src, g, j0, c0):
+            rows = src[g * K_PASS : (g + 1) * K_PASS, :].rearrange("(p j) c -> p j c", j=PACK)
+            nc.sync.dma_start(out=raw[:], in_=rows[:, j0 : j0 + raw.shape[1], c0 : c0 + raw.shape[2]])
             return raw
 
-        x_raw = {}
-        x_raw[0, 0] = [(load_rows(xT, 0, 0, 2, 0, T, "x_raw_00"), 0, T, WHOLE_ON_SCALAR)]
+        def load_row_pair(g, u):
+            parts, c0 = [], 0
+            for width, on_scalar in X_LOADS[2 * g + u]:
+                raw = held([P, 2, width], F32, "x_raw_%d%d_%d" % (g, u, c0))
+                parts.append((load_rows(raw, xT, g, 2 * u, c0), c0, width, on_scalar))
+                c0 = c0 + width
+            return parts
+
+        def load_words(i, words):
+            tile = held([P, 2 * N], U8, "w23_words_%d" % i)
+            nc.sync.dma_start(out=tile[:].bitcast(I32), in_=words[0].bitcast(I32))
+            return tile
+
+        x_raw = {(0, 0): load_row_pair(0, 0)}
         nc.sync.dma_start(offsets[:], offs)
-        x_raw[0, 1] = [
-            (load_rows(xT, 0, 2, 2, 0, T // 2, "x_raw_01_0"), 0, T // 2, T // 2),
-            (load_rows(xT, 0, 2, 2, T // 2, T // 2, "x_raw_01_1"), T // 2, T // 2, 320),
-        ]
-        w1_raw0 = load_rows(w1, 0, 0, PACK, 0, H, "w1_raw0")
-        x_raw[1, 0] = [
-            (load_rows(xT, 1, 0, 2, 0, T // 2, "x_raw_10_0"), 0, T // 2, T // 2),
-            (load_rows(xT, 1, 0, 2, T // 2, T // 2, "x_raw_10_1"), T // 2, T // 2, 320),
-        ]
-        x_raw[1, 1] = []
-        c0 = 0
-        for width, on_scalar in LAST_LOADS:
-            x_raw[1, 1].append((load_rows(xT, 1, 2, 2, c0, width, "x_raw_11_%d" % c0), c0, width, on_scalar))
-            c0 = c0 + width
-        w1_raw1, w23_words = [], []
-        for i, words in enumerate((w2_words, w3_words)):
-            w1_raw1.append(load_rows(w1, 1, 0, PACK, i * H // 2, H // 2, "w1_raw1_%d" % i))
-            w23_words.append(held([P, 2 * N], U8, "w23_words_%d" % i))
-            nc.sync.dma_start(out=w23_words[i][:].bitcast(I32), in_=words[0].bitcast(I32))
+        x_raw[0, 1] = load_row_pair(0, 1)
+        w1_raw0 = load_rows(held([P, PACK, H], F32, "w1_raw0"), w1, 0, 0, 0)
+        x_raw[1, 0] = load_row_pair(1, 0)
+        x_raw[1, 1] = load_row_pair(1, 1)
+        first, second, last = W1_LOADS
+        w1_raw1 = [load_rows(held([P, PACK, first], F32, "w1_raw1_first"), w1, 1, 0, 0)]
+        w23_words = [load_words(0, w2_words)]
+        w1_raw1.append(load_rows(held([P, PACK, second], F32, "w1_raw1_second"), w1, 1, 0, first))
+        w1_raw1.append(load_rows(placed([P, PACK, last], F32, "w1_raw1_last", 0), w1, 1, 0, first + second))
+        w23_words.append(load_words(1, w3_words))
         for i, scales in enumerate((w2_scales, w3_scales)):
             for q in range(P // 32):
                 nc.sync.dma_start(
@@ -89,28 +102,28 @@ def tile_picked_haar_gelu_e_kernel(
         picked = [held([P, 2 * S], U32, "picked_%d" % g) for g in range(2)]
 
         def pick(g, u):
-            pairs = held([P, 2 * T], BF16, "x_pairs_%d%d" % (g, u))
-            dst = pairs[:].rearrange("p (c r j) -> p c j r", r=RUN, j=2)
+            rounded = held([P, 2 * T], BF16, "x_rounded_%d%d" % (g, u))
+            dst = rounded[:].rearrange("p (c r j) -> p c j r", r=RUN, j=2)
             for raw, c0, width, on_scalar in x_raw[g, u]:
                 src = raw[:].rearrange("p j (c r) -> p c j r", r=RUN)
-                a, b, c = c0 // RUN, on_scalar // RUN, width // RUN
-                if b > 0:
-                    nc.scalar.activation(dst[:, a : a + b], src[:, :b], ACT.Copy)
-                if b < c:
-                    nc.vector.tensor_copy(out=dst[:, a + b : a + c], in_=src[:, b:])
+                start, split, runs = c0 // RUN, on_scalar // RUN, width // RUN
+                if split > 0:
+                    nc.scalar.activation(dst[:, start : start + split], src[:, :split], ACT.Copy)
+                if split < runs:
+                    nc.vector.tensor_copy(out=dst[:, start + split : start + runs], in_=src[:, split:])
             by_bank = picked[g][:, u * S : (u + 1) * S].rearrange("p (b d c) -> p d b c", d=PIECES, c=GROUP)
-            nc.vector.tensor_copy(by_bank, pairs[:].bitcast(U32).indirect(offsets[:]))
+            nc.vector.tensor_copy(by_bank, rounded[:].bitcast(U32).indirect(offsets[:]))
+
+        def weave_views(woven, g, b0, b1, dtype):
+            src = picked[g][:].bitcast(dtype).rearrange("p (u c r) -> p c u r", u=2, r=2)
+            dst = woven.bitcast(dtype).rearrange("p (c r u) -> p c u r", u=2, r=2)
+            return dst, src[:, b0 * P // 2 : b1 * P // 2]
 
         x_mx = {}
 
-        def weave_views(g, half, woven, dtype):
-            src = picked[g][:].bitcast(dtype).rearrange("p (u c r) -> p c u r", u=2, r=2)
-            dst = woven[:].bitcast(dtype).rearrange("p (c r u) -> p c u r", u=2, r=2)
-            return dst, src[:, half * S // 4 : (half + 1) * S // 4]
-
-        def quantize_x(g, b0, banks, woven, name, tag=None):
-            codes = held([P, banks * P], U32, name, tag=tag)
-            scales = held([P, banks * P], U8, name + "_scales")
+        def quantize_x(codes, g, b0, woven):
+            banks = codes.shape[1] // P
+            scales = held([P, banks * P], U8, "x_scales_%d%d" % (g, b0))
             nc.vector.quantize_mx(out=codes[:].bitcast(FP8X4), scales=scales[:], in_=woven)
             for b in range(banks):
                 x_mx[g, b0 + b] = (codes[:, b * P : (b + 1) * P], scales[:, b * P : (b + 1) * P])
@@ -124,60 +137,65 @@ def tile_picked_haar_gelu_e_kernel(
         def by_channel(raw):
             return raw[:].rearrange("p j (m t) -> p m j t", t=PACK)
 
+        def quantize_w1(g, grouped, t0, t1):
+            cols = slice(t0 * P, t1 * P)
+            nc.vector.quantize_mx(
+                out=w1_codes[g][:, cols].bitcast(FP8X4),
+                scales=w1_scales[g][:, cols],
+                in_=grouped[:, t0 * P * PACK : t1 * P * PACK],
+            )
+
         pick(0, 0)
         pick(0, 1)
         w1_bf0 = held([P, PACK * H], BF16, "w1_bf0")
         nc.scalar.activation(dealt(w1_bf0), by_channel(w1_raw0), ACT.Copy)
-        woven0 = [held([P, PACK * S // 2], BF16, "woven_00"), held([P, PACK * S // 2], BF16, "woven_01")]
-        dst, src = weave_views(0, 0, woven0[0], I32)
-        nc.vector.tensor_copy(out=dst, in_=src)
-        dst, src = weave_views(0, 1, woven0[1], I32)
-        nc.vector.tensor_copy(out=dst, in_=src)
-        quantize_x(0, 0, 4, woven0[0][:], "x_codes_00")
-        quantize_x(0, 4, 4, woven0[1][:], "x_codes_04")
-        nc.vector.quantize_mx(out=w1_codes[0][:].bitcast(FP8X4), scales=w1_scales[0][:], in_=w1_bf0[:])
+        halves = (0, BANKS // 2)
+        woven0 = [held([P, BANKS // 2 * BAND], BF16, "woven0_%d" % b0) for b0 in halves]
+        for woven, b0 in zip(woven0, halves):
+            nc.vector.tensor_copy(*weave_views(woven[:], 0, b0, b0 + BANKS // 2, I32))
+        for woven, b0 in zip(woven0, halves):
+            quantize_x(held([P, BANKS // 2 * P], U32, "x_codes_0%d" % b0), 0, b0, woven[:])
+        quantize_w1(0, w1_bf0, 0, PACK)
 
         pick(1, 0)
         pick(1, 1)
-        woven10 = held([P, PACK * S // 2], BF16, "woven_10")
-        dst, src = weave_views(1, 0, woven10, I32)
-        nc.vector.tensor_copy(out=dst[:, :P], in_=src[:, :P])
-        nc.vector.tensor_copy(out=dst[:, P:], in_=src[:, P:])
-        quantize_x(1, 0, 2, woven10[:, : PACK * 2 * P], "x_codes_10")
+        woven_first = held([P, VECTOR_BANKS * BAND], BF16, "woven_first")
+        nc.vector.tensor_copy(*weave_views(woven_first[:], 1, 0, VECTOR_BANKS, I32))
 
         warm_up = psum.tile([P, H], F32, name="warm_up", tag="bank%d" % (BANKS - 1))
-        for i, passes in enumerate(WARM_UP_PASSES):
-            for repeat in range(passes):
-                nc.tensor.matmul_mx(
-                    out=warm_up[:],
-                    lhsT=w23_words[i][:, : 2 * P].bitcast(FP4X4),
-                    lhsT_scale=w1_scales[0][:, :P],
-                    rhs=w1_codes[0][:].bitcast(FP8X4),
-                    rhs_scale=w1_scales[0][:],
-                    start=True,
-                    stop=True,
-                )
-
-        w1_bf1 = held([P, PACK * H], BF16, "w1_bf1")
-        for u in range(2):
-            nc.scalar.activation(dealt(w1_bf1)[:, u * P // 2 : (u + 1) * P // 2], by_channel(w1_raw1[u]), ACT.Copy)
-        for u in range(2):
-            cols = slice(u * H // 2, (u + 1) * H // 2)
-            nc.vector.quantize_mx(
-                out=w1_codes[1][:, cols].bitcast(FP8X4),
-                scales=w1_scales[1][:, cols],
-                in_=w1_bf1[:, u * PACK * H // 2 : (u + 1) * PACK * H // 2],
+        for repeat in range(WARM_UP_PASSES):
+            nc.tensor.matmul_mx(
+                out=warm_up[:],
+                lhsT=w23_words[0][:, : 2 * P].bitcast(FP4X4),
+                lhsT_scale=w1_scales[0][:, :P],
+                rhs=w1_codes[0][:].bitcast(FP8X4),
+                rhs_scale=w1_scales[0][:],
+                start=True,
+                stop=True,
             )
 
-        quantize_x(1, 2, 2, woven10[:, PACK * 2 * P :], "x_codes_12", tag="w1_bf1")
-        woven11 = held([P, PACK * S // 2], BF16, "woven_11", tag="w1_raw1_1")
-        dst, src = weave_views(1, 1, woven11, U32)
-        nc.scalar.copy(dst, src)
-        quantize_x(1, 4, 4, woven11[:], "x_codes_14")
+        w1_bf1 = held([P, PACK * H], BF16, "w1_bf1")
+        m0 = 0
+        for raw in w1_raw1:
+            m1 = m0 + raw.shape[2] // PACK
+            nc.scalar.activation(dealt(w1_bf1)[:, m0:m1], by_channel(raw), ACT.Copy)
+            m0 = m1
 
-        h = [held([P, 2, PIECES, BAND // 2], F32, "h_%d" % s) for s in range(V // SLICE)]
+        first_codes = placed([P, VECTOR_BANKS * P], U32, "x_codes_10", 0)
+        woven_rest = placed([P, (BANKS - VECTOR_BANKS) * BAND], BF16, "woven_rest", 4 * VECTOR_BANKS * P)
+        next_banks = BANKS // 2 - VECTOR_BANKS
+        woven_next, woven_last = woven_rest[:, : next_banks * BAND], woven_rest[:, next_banks * BAND :]
+        nc.scalar.copy(*weave_views(woven_next, 1, VECTOR_BANKS, BANKS // 2, U32))
+        nc.scalar.copy(*weave_views(woven_last, 1, BANKS // 2, BANKS, U32))
+        quantize_w1(1, w1_bf1, 0, PACK // 2)
+        quantize_x(first_codes, 1, 0, woven_first[:])
+        quantize_w1(1, w1_bf1, PACK // 2, PACK)
+        quantize_x(held([P, next_banks * P], U32, "x_codes_1_next"), 1, VECTOR_BANKS, woven_next)
+        quantize_x(held([P, BANKS // 2 * P], U32, "x_codes_1_last"), 1, BANKS // 2, woven_last)
 
-        def hidden(b):
+        slices = V // SLICE
+        h = [held([P, 2, PIECES, GROUP * PACK], F32, "h_%d" % s) for s in range(slices)]
+        for b in range(BANKS):
             bank = psum.tile([P, PACK, P], F32, name="h_bank_%d" % b, tag="bank%d" % b)
             for t in range(PACK):
                 m_cols = slice(t * P, (t + 1) * P)
@@ -192,15 +210,17 @@ def tile_picked_haar_gelu_e_kernel(
                         stop=(g == 1),
                     )
             nc.scalar.activation(
-                h[b // 2][:, b % 2].rearrange("p d (v t) -> p (d v) t", t=PACK),
+                h[b // 2][:, b % 2].rearrange("p d (c t) -> p (d c) t", t=PACK),
                 bank[:].rearrange("p t v -> p v t"),
                 ACT.Gelu_apprx_tanh,
             )
 
-        def band(s, i, b0, b1):
-            op = ALU.add if i == 0 else ALU.subtract
+        bands = [held([P, 2 * BAND], BF16, "bands_%d" % s) for s in range(slices)]
+
+        def band(s, i, of_banks=slice(0, 2)):
             dst = bands[s][:, i * BAND : (i + 1) * BAND].rearrange("p (b x) -> p b x", b=2)
-            nc.vector.tensor_tensor(dst[:, b0:b1], h[s][:, b0:b1, 0], h[s][:, b0:b1, 1], op)
+            op = ALU.add if i == 0 else ALU.subtract
+            nc.vector.tensor_tensor(dst[:, of_banks], h[s][:, of_banks, 0], h[s][:, of_banks, 1], op)
 
         def band_pass(acc, mt, i, codes, scales):
             nc.tensor.matmul_mx(
@@ -213,11 +233,11 @@ def tile_picked_haar_gelu_e_kernel(
                 stop=(i == 1),
             )
 
-        def finish(s, both):
+        def finish(s):
             codes = held([P, 2 * SLICE], U32, "band_codes_%d" % s)
             scales = held([P, 2 * SLICE], U8, "band_scales_%d" % s)
-            nc.vector.quantize_mx(out=codes[:].bitcast(FP8X4), scales=scales[:], in_=both[:])
-            acc = psum.tile([P, 2, SLICE], F32, name="acc_%d" % s, tag="bank%d" % (5 + s))
+            nc.vector.quantize_mx(out=codes[:].bitcast(FP8X4), scales=scales[:], in_=bands[s][:])
+            acc = psum.tile([P, 2, SLICE], F32, name="acc_%d" % s, tag="bank%d" % (BANKS - slices + 1 + s))
             for mt in range(N // P):
                 for i in range(2):
                     cols = slice(i * SLICE, (i + 1) * SLICE)
@@ -228,13 +248,13 @@ def tile_picked_haar_gelu_e_kernel(
                 out=out[:, s * SLICE : (s + 1) * SLICE].rearrange("(mt p) v -> p mt v", p=P), in_=result[:]
             )
 
-        def finish_last(s, both):
+        def finish_last(s):
             accs = [psum.tile([P, SLICE], F32, name="acc_last_%d" % mt, tag="bank%d" % mt) for mt in range(N // P)]
             for i in range(2):
                 codes = held([P, SLICE], U32, "last_codes_%d" % i)
                 scales = held([P, SLICE], U8, "last_scales_%d" % i)
                 nc.vector.quantize_mx(
-                    out=codes[:].bitcast(FP8X4), scales=scales[:], in_=both[:, i * BAND : (i + 1) * BAND]
+                    out=codes[:].bitcast(FP8X4), scales=scales[:], in_=bands[s][:, i * BAND : (i + 1) * BAND]
                 )
                 for mt in range(N // P):
                     band_pass(accs[mt][:], mt, i, codes[:], scales[:])
@@ -245,15 +265,11 @@ def tile_picked_haar_gelu_e_kernel(
             nc.scalar.activation(results[1][:], accs[1][:], ACT.Copy, scale=0.5)
             nc.scalar.dma_start(out=out[P:, cols], in_=results[1][:])
 
-        slices = V // SLICE
-        for b in range(BANKS):
-            hidden(b)
-        bands = [held([P, 2 * BAND], BF16, "bands_%d" % s) for s in range(slices)]
         for b in range(2):
             for i in range(2):
-                band(0, i, b, b + 1)
+                band(0, i, slice(b, b + 1))
         for s in range(1, slices):
-            band(s, 0, 0, 2)
-            finish(s - 1, bands[s - 1])
-            band(s, 1, 0, 2)
-        finish_last(slices - 1, bands[slices - 1])
+            band(s, 0)
+            finish(s - 1)
+            band(s, 1)
+        finish_last(slices - 1)

@@ -27,15 +27,14 @@ GROUP = 64
 BANKS = 8
 SLICE = 128
 BAND = SLICE * PACK
-X_LOADS = (
-    ((2048, 672),),
-    ((1024, 1024), (1024, 320)),
-    ((1024, 1024), (1024, 320)),
-    ((1024, 1024), (512, 0), (512, 128)),
+X_STEPS = (
+    ((1280, 432), (2048, 256)),
+    ((1280, 432), (2048, 256)),
+    ((1024, 1024), (2048, 0)),
 )
-W1_LOADS = (192, 192, 128)
+LAST_STEPS = ((512, 0), (1024, 160))
 VECTOR_BANKS = 2
-WARM_UP_PASSES = 5
+WARM_UP_PASSES = (2, 3)
 
 
 def tile_picked_haar_gelu_e_kernel(
@@ -68,12 +67,25 @@ def tile_picked_haar_gelu_e_kernel(
             return raw
 
         def load_row_pair(g, u):
-            parts, c0 = [], 0
-            for width, on_scalar in X_LOADS[2 * g + u]:
-                raw = held([P, 2, width], F32, "x_raw_%d%d_%d" % (g, u, c0))
-                parts.append((load_rows(raw, xT, g, 2 * u, c0), c0, width, on_scalar))
-                c0 = c0 + width
-            return parts
+            raw = held([P, 2 * T], F32, "x_raw_%d%d" % (g, u))
+            run = xT[g * K_PASS : (g + 1) * K_PASS, :].rearrange("(p j) c -> p (j c)", j=PACK)
+            done = 0
+            for c1, on_scalar in X_STEPS[2 * g + u]:
+                nc.sync.dma_start(out=raw[:, done : T + c1], in_=run[:, 2 * T * u + done : 2 * T * u + T + c1])
+                done = T + c1
+            return [(raw[:].rearrange("p (j c) -> p j c", j=2), 0, X_STEPS[2 * g + u])]
+
+        def load_last_row_pair():
+            half = T // 2
+            first = load_rows(held([P, 2, half], F32, "x_raw_11_first"), xT, 1, 2, 0)
+            raw = held([P, 2 * half], F32, "x_raw_11_second")
+            rows = xT[K_PASS:, half:].rearrange("(p j) c -> p j c", j=PACK)
+            nc.sync.dma_start(out=raw[:, :half], in_=rows[:, 2])
+            done = 0
+            for c1, on_scalar in LAST_STEPS:
+                nc.sync.dma_start(out=raw[:, half + done : half + c1], in_=rows[:, 3, done:c1])
+                done = c1
+            return [(first[:], 0, ((half, half),)), (raw[:].rearrange("p (j c) -> p j c", j=2), half, LAST_STEPS)]
 
         def load_words(i, words):
             tile = held([P, 2 * N], U8, "w23_words_%d" % i)
@@ -85,13 +97,12 @@ def tile_picked_haar_gelu_e_kernel(
         x_raw[0, 1] = load_row_pair(0, 1)
         w1_raw0 = load_rows(held([P, PACK, H], F32, "w1_raw0"), w1, 0, 0, 0)
         x_raw[1, 0] = load_row_pair(1, 0)
-        x_raw[1, 1] = load_row_pair(1, 1)
-        first, second, last = W1_LOADS
-        w1_raw1 = [load_rows(held([P, PACK, first], F32, "w1_raw1_first"), w1, 1, 0, 0)]
-        w23_words = [load_words(0, w2_words)]
-        w1_raw1.append(load_rows(held([P, PACK, second], F32, "w1_raw1_second"), w1, 1, 0, first))
-        w1_raw1.append(load_rows(placed([P, PACK, last], F32, "w1_raw1_last", 0), w1, 1, 0, first + second))
-        w23_words.append(load_words(1, w3_words))
+        x_raw[1, 1] = load_last_row_pair()
+        w1_raw1 = [held([P, PACK, H // 2], F32, "w1_raw1_0"), placed([P, PACK, H // 2], F32, "w1_raw1_1", 0)]
+        w23_words = []
+        for i, words in enumerate((w2_words, w3_words)):
+            load_rows(w1_raw1[i], w1, 1, 0, i * H // 2)
+            w23_words.append(load_words(i, words))
         for i, scales in enumerate((w2_scales, w3_scales)):
             for q in range(P // 32):
                 nc.sync.dma_start(
@@ -104,13 +115,16 @@ def tile_picked_haar_gelu_e_kernel(
         def pick(g, u):
             rounded = held([P, 2 * T], BF16, "x_rounded_%d%d" % (g, u))
             dst = rounded[:].rearrange("p (c r j) -> p c j r", r=RUN, j=2)
-            for raw, c0, width, on_scalar in x_raw[g, u]:
-                src = raw[:].rearrange("p j (c r) -> p c j r", r=RUN)
-                start, split, runs = c0 // RUN, on_scalar // RUN, width // RUN
-                if split > 0:
-                    nc.scalar.activation(dst[:, start : start + split], src[:, :split], ACT.Copy)
-                if split < runs:
-                    nc.vector.tensor_copy(out=dst[:, start + split : start + runs], in_=src[:, split:])
+            for raw, base, steps in x_raw[g, u]:
+                src = raw.rearrange("p j (c r) -> p c j r", r=RUN)
+                start = 0
+                for c1, on_scalar in steps:
+                    split, end = start + on_scalar // RUN, c1 // RUN
+                    if split > start:
+                        nc.scalar.activation(dst[:, base // RUN :][:, start:split], src[:, start:split], ACT.Copy)
+                    if split < end:
+                        nc.vector.tensor_copy(out=dst[:, base // RUN :][:, split:end], in_=src[:, split:end])
+                    start = end
             by_bank = picked[g][:, u * S : (u + 1) * S].rearrange("p (b d c) -> p d b c", d=PIECES, c=GROUP)
             nc.vector.tensor_copy(by_bank, rounded[:].bitcast(U32).indirect(offsets[:]))
 
@@ -163,16 +177,17 @@ def tile_picked_haar_gelu_e_kernel(
         nc.vector.tensor_copy(*weave_views(woven_first[:], 1, 0, VECTOR_BANKS, I32))
 
         warm_up = psum.tile([P, H], F32, name="warm_up", tag="bank%d" % (BANKS - 1))
-        for repeat in range(WARM_UP_PASSES):
-            nc.tensor.matmul_mx(
-                out=warm_up[:],
-                lhsT=w23_words[0][:, : 2 * P].bitcast(FP4X4),
-                lhsT_scale=w1_scales[0][:, :P],
-                rhs=w1_codes[0][:].bitcast(FP8X4),
-                rhs_scale=w1_scales[0][:],
-                start=True,
-                stop=True,
-            )
+        for i, passes in enumerate(WARM_UP_PASSES):
+            for repeat in range(passes):
+                nc.tensor.matmul_mx(
+                    out=warm_up[:],
+                    lhsT=w23_words[i][:, : 2 * P].bitcast(FP4X4),
+                    lhsT_scale=w1_scales[0][:, :P],
+                    rhs=w1_codes[0][:].bitcast(FP8X4),
+                    rhs_scale=w1_scales[0][:],
+                    start=True,
+                    stop=True,
+                )
 
         w1_bf1 = held([P, PACK * H], BF16, "w1_bf1")
         m0 = 0

@@ -25,6 +25,7 @@ SCALE_ROWS = 4
 RUN = 4
 GROUP = 64
 BANKS = 8
+EARLY_BANKS = 2 * N // P
 SLICE = 128
 BAND = SLICE * PACK
 X_STEPS = (
@@ -34,7 +35,6 @@ X_STEPS = (
 )
 LAST_STEPS = ((512, 0), (1024, 160))
 VECTOR_BANKS = 2
-WARM_UP_PASSES = (2, 3)
 
 
 def tile_picked_haar_gelu_e_kernel(
@@ -54,8 +54,9 @@ def tile_picked_haar_gelu_e_kernel(
 
         offsets = keep.tile([P, S // LIST_ROWS], U16, name="offsets")
 
-        w23_scales = held([P, 2 * N], U8, "w23_scales")
-        nc.vector.memset(w23_scales[:].bitcast(I32), 0)
+        two_planes = held([P, 2 * N], U8, "two_planes")
+        nc.vector.memset(two_planes[:].bitcast(I32), 0)
+        w23_scales = [two_planes[:, :N], two_planes[:, N:]]
 
         table_warm = held([P, 2], F32, "table_warm")
         nc.vector.memset(table_warm[:, :1], 0.0)
@@ -98,15 +99,11 @@ def tile_picked_haar_gelu_e_kernel(
         w1_raw0 = load_rows(held([P, PACK, H], F32, "w1_raw0"), w1, 0, 0, 0)
         x_raw[1, 0] = load_row_pair(1, 0)
         x_raw[1, 1] = load_last_row_pair()
-        w1_raw1 = [held([P, PACK, H // 2], F32, "w1_raw1_0"), placed([P, PACK, H // 2], F32, "w1_raw1_1", 0)]
-        w23_words = []
-        for i, words in enumerate((w2_words, w3_words)):
-            load_rows(w1_raw1[i], w1, 1, 0, i * H // 2)
-            w23_words.append(load_words(i, words))
-        for i, scales in enumerate((w2_scales, w3_scales)):
-            for q in range(P // 32):
+
+        def load_scales(i, scales, groups):
+            for q in groups:
                 nc.sync.dma_start(
-                    out=w23_scales[32 * q : 32 * q + SCALE_ROWS, N * i : N * (i + 1)].bitcast(I32),
+                    out=w23_scales[i][32 * q : 32 * q + SCALE_ROWS, :].bitcast(I32),
                     in_=scales[0, SCALE_ROWS * q : SCALE_ROWS * (q + 1), :].bitcast(I32),
                 )
 
@@ -135,11 +132,9 @@ def tile_picked_haar_gelu_e_kernel(
 
         x_mx = {}
 
-        def quantize_x(codes, g, b0, woven):
-            banks = codes.shape[1] // P
-            scales = held([P, banks * P], U8, "x_scales_%d%d" % (g, b0))
-            nc.vector.quantize_mx(out=codes[:].bitcast(FP8X4), scales=scales[:], in_=woven)
-            for b in range(banks):
+        def quantize_x(codes, scales, g, b0, woven):
+            nc.vector.quantize_mx(out=codes[:].bitcast(FP8X4), scales=scales, in_=woven)
+            for b in range(codes.shape[1] // P):
                 x_mx[g, b0 + b] = (codes[:, b * P : (b + 1) * P], scales[:, b * P : (b + 1) * P])
 
         w1_codes = [held([P, H], U32, "w1_codes_%d" % g) for g in range(2)]
@@ -163,31 +158,45 @@ def tile_picked_haar_gelu_e_kernel(
         pick(0, 1)
         w1_bf0 = held([P, PACK * H], BF16, "w1_bf0")
         nc.scalar.activation(dealt(w1_bf0), by_channel(w1_raw0), ACT.Copy)
-        halves = (0, BANKS // 2)
+        halves = (0, EARLY_BANKS)
         woven0 = [held([P, BANKS // 2 * BAND], BF16, "woven0_%d" % b0) for b0 in halves]
+        scales0 = [two_planes[SCALE_ROWS:, :], held([P, BANKS // 2 * P], U8, "x_scales_0_late")[:]]
         for woven, b0 in zip(woven0, halves):
             nc.vector.tensor_copy(*weave_views(woven[:], 0, b0, b0 + BANKS // 2, I32))
-        for woven, b0 in zip(woven0, halves):
-            quantize_x(held([P, BANKS // 2 * P], U32, "x_codes_0%d" % b0), 0, b0, woven[:])
+        for woven, scales, b0 in zip(woven0, scales0, halves):
+            quantize_x(held([P, BANKS // 2 * P], U32, "x_codes_0%d" % b0), scales, 0, b0, woven[:])
         quantize_w1(0, w1_bf0, 0, PACK)
+
+        w1_raw1 = [held([P, PACK, H // 2], F32, "w1_raw1_0"), placed([P, PACK, H // 2], F32, "w1_raw1_1", 0)]
+        for i, scales in enumerate((w2_scales, w3_scales)):
+            load_rows(w1_raw1[i], w1, 1, 0, i * H // 2)
+            load_scales(i, scales, (1,))
+        w23_words = [load_words(i, words) for i, words in enumerate((w2_words, w3_words))]
+
+        banks = [psum.tile([P, PACK, P], F32, name="h_bank_%d" % b, tag="bank%d" % b) for b in range(BANKS)]
+
+        def first_pass(g, b, t, start, stop):
+            m_cols = slice(t * P, (t + 1) * P)
+            nc.tensor.matmul_mx(
+                out=banks[b][:, t, :],
+                lhsT=w1_codes[g][:, m_cols].bitcast(FP8X4),
+                lhsT_scale=w1_scales[g][:, m_cols],
+                rhs=x_mx[g, b][0].bitcast(FP8X4),
+                rhs_scale=x_mx[g, b][1],
+                start=start,
+                stop=stop,
+            )
+
+        for b in range(EARLY_BANKS):
+            for t in range(PACK):
+                first_pass(0, b, t, t == 0, False)
+        for i, scales in enumerate((w2_scales, w3_scales)):
+            load_scales(i, scales, (0, 2, 3))
 
         pick(1, 0)
         pick(1, 1)
         woven_first = held([P, VECTOR_BANKS * BAND], BF16, "woven_first")
         nc.vector.tensor_copy(*weave_views(woven_first[:], 1, 0, VECTOR_BANKS, I32))
-
-        warm_up = psum.tile([P, H], F32, name="warm_up", tag="bank%d" % (BANKS - 1))
-        for i, passes in enumerate(WARM_UP_PASSES):
-            for repeat in range(passes):
-                nc.tensor.matmul_mx(
-                    out=warm_up[:],
-                    lhsT=w23_words[i][:, : 2 * P].bitcast(FP4X4),
-                    lhsT_scale=w1_scales[0][:, :P],
-                    rhs=w1_codes[0][:].bitcast(FP8X4),
-                    rhs_scale=w1_scales[0][:],
-                    start=True,
-                    stop=True,
-                )
 
         w1_bf1 = held([P, PACK * H], BF16, "w1_bf1")
         m0 = 0
@@ -203,30 +212,25 @@ def tile_picked_haar_gelu_e_kernel(
         nc.scalar.copy(*weave_views(woven_next, 1, VECTOR_BANKS, BANKS // 2, U32))
         nc.scalar.copy(*weave_views(woven_last, 1, BANKS // 2, BANKS, U32))
         quantize_w1(1, w1_bf1, 0, PACK // 2)
-        quantize_x(first_codes, 1, 0, woven_first[:])
+        quantize_x(first_codes, held([P, VECTOR_BANKS * P], U8, "x_scales_1_first")[:], 1, 0, woven_first[:])
         quantize_w1(1, w1_bf1, PACK // 2, PACK)
-        quantize_x(held([P, next_banks * P], U32, "x_codes_1_next"), 1, VECTOR_BANKS, woven_next)
-        quantize_x(held([P, BANKS // 2 * P], U32, "x_codes_1_last"), 1, BANKS // 2, woven_last)
+        for b0, woven in ((VECTOR_BANKS, woven_next), (BANKS // 2, woven_last)):
+            width = woven.shape[1] // PACK
+            codes, scales = held([P, width], U32, "x_codes_1%d" % b0), held([P, width], U8, "x_scales_1%d" % b0)
+            quantize_x(codes, scales[:], 1, b0, woven)
 
         slices = V // SLICE
         h = [held([P, 2, PIECES, GROUP * PACK], F32, "h_%d" % s) for s in range(slices)]
         for b in range(BANKS):
-            bank = psum.tile([P, PACK, P], F32, name="h_bank_%d" % b, tag="bank%d" % b)
             for t in range(PACK):
-                m_cols = slice(t * P, (t + 1) * P)
-                for g in range(2):
-                    nc.tensor.matmul_mx(
-                        out=bank[:, t, :],
-                        lhsT=w1_codes[g][:, m_cols].bitcast(FP8X4),
-                        lhsT_scale=w1_scales[g][:, m_cols],
-                        rhs=x_mx[g, b][0].bitcast(FP8X4),
-                        rhs_scale=x_mx[g, b][1],
-                        start=(g == 0),
-                        stop=(g == 1),
-                    )
+                if b < EARLY_BANKS:
+                    first_pass(1, b, t, False, t == PACK - 1)
+                else:
+                    first_pass(0, b, t, True, False)
+                    first_pass(1, b, t, False, True)
             nc.scalar.activation(
                 h[b // 2][:, b % 2].rearrange("p d (c t) -> p (d c) t", t=PACK),
-                bank[:].rearrange("p t v -> p v t"),
+                banks[b][:].rearrange("p t v -> p v t"),
                 ACT.Gelu_apprx_tanh,
             )
 
@@ -241,7 +245,7 @@ def tile_picked_haar_gelu_e_kernel(
             nc.tensor.matmul_mx(
                 out=acc,
                 lhsT=w23_words[i][:, 2 * P * mt : 2 * P * (mt + 1)].bitcast(FP4X4),
-                lhsT_scale=w23_scales[:, N * i + P * mt : N * i + P * (mt + 1)],
+                lhsT_scale=w23_scales[i][:, P * mt : P * (mt + 1)],
                 rhs=codes.bitcast(FP8X4),
                 rhs_scale=scales,
                 start=(i == 0),

@@ -33,7 +33,10 @@ X_STEPS = (
     ((1280, 432), (2048, 256)),
     ((1024, 1024), (2048, 0)),
 )
-LAST_STEPS = ((512, 0), (1024, 160))
+LAST_FIRST = 896
+LAST_STEPS = ((576, 240), (1152, 192))
+W1_PLACES = (4096, 0)
+WOVEN_REST_PLACE = 8192
 VECTOR_BANKS = 2
 
 
@@ -77,16 +80,22 @@ def tile_picked_haar_gelu_e_kernel(
             return [(raw[:].rearrange("p (j c) -> p j c", j=2), 0, X_STEPS[2 * g + u])]
 
         def load_last_row_pair():
-            half = T // 2
-            first = load_rows(held([P, 2, half], F32, "x_raw_11_first"), xT, 1, 2, 0)
-            raw = held([P, 2 * half], F32, "x_raw_11_second")
-            rows = xT[K_PASS:, half:].rearrange("(p j) c -> p j c", j=PACK)
-            nc.sync.dma_start(out=raw[:, :half], in_=rows[:, 2])
+            rest = T - LAST_FIRST
+            first = load_rows(held([P, 2, LAST_FIRST], F32, "x_raw_11_first"), xT, 1, 2, 0)
+            raw = held([P, 2 * rest], F32, "x_raw_11_second")
+            rows = xT[K_PASS:, LAST_FIRST:].rearrange("(p j) c -> p j c", j=PACK)
+            nc.sync.dma_start(out=raw[:, :rest], in_=rows[:, 2])
             done = 0
             for c1, on_scalar in LAST_STEPS:
-                nc.sync.dma_start(out=raw[:, half + done : half + c1], in_=rows[:, 3, done:c1])
+                nc.sync.dma_start(out=raw[:, rest + done : rest + c1], in_=rows[:, 3, done:c1])
                 done = c1
-            return [(first[:], 0, ((half, half),)), (raw[:].rearrange("p (j c) -> p j c", j=2), half, LAST_STEPS)]
+            second = raw[:].rearrange("p (j c) -> p j c", j=2)
+            return [(first[:], 0, ((LAST_FIRST, LAST_FIRST),)), (second, LAST_FIRST, LAST_STEPS)]
+
+        def load_w1_half(g, i):
+            shape, name = [P, PACK, H // 2], "w1_raw%d_%d" % (g, i)
+            raw = placed(shape, F32, name, W1_PLACES[g]) if i else held(shape, F32, name)
+            return load_rows(raw, w1, g, 0, i * H // 2)
 
         def load_words(i, words):
             tile = held([P, 2 * N], U8, "w23_words_%d" % i)
@@ -96,7 +105,7 @@ def tile_picked_haar_gelu_e_kernel(
         x_raw = {(0, 0): load_row_pair(0, 0)}
         nc.sync.dma_start(offsets[:], offs)
         x_raw[0, 1] = load_row_pair(0, 1)
-        w1_raw0 = load_rows(held([P, PACK, H], F32, "w1_raw0"), w1, 0, 0, 0)
+        w1_raw0 = [load_w1_half(0, i) for i in range(2)]
         x_raw[1, 0] = load_row_pair(1, 0)
         x_raw[1, 1] = load_last_row_pair()
 
@@ -109,7 +118,7 @@ def tile_picked_haar_gelu_e_kernel(
 
         picked = [held([P, 2 * S], U32, "picked_%d" % g) for g in range(2)]
 
-        def pick(g, u):
+        def pick(g, u, cuts=(S,)):
             rounded = held([P, 2 * T], BF16, "x_rounded_%d%d" % (g, u))
             dst = rounded[:].rearrange("p (c r j) -> p c j r", r=RUN, j=2)
             for raw, base, steps in x_raw[g, u]:
@@ -122,13 +131,16 @@ def tile_picked_haar_gelu_e_kernel(
                     if split < end:
                         nc.vector.tensor_copy(out=dst[:, base // RUN :][:, split:end], in_=src[:, split:end])
                     start = end
-            by_bank = picked[g][:, u * S : (u + 1) * S].rearrange("p (b d c) -> p d b c", d=PIECES, c=GROUP)
-            nc.vector.tensor_copy(by_bank, rounded[:].bitcast(U32).indirect(offsets[:]))
+            e0 = 0
+            for e1 in cuts:
+                window = rounded[:].bitcast(U32).indirect(offsets[:, e0 // LIST_ROWS : e1 // LIST_ROWS])
+                nc.vector.tensor_copy(picked[g][:, u * S + e0 : u * S + e1], window)
+                e0 = e1
 
         def weave_views(woven, g, b0, b1, dtype):
-            src = picked[g][:].bitcast(dtype).rearrange("p (u c r) -> p c u r", u=2, r=2)
-            dst = woven.bitcast(dtype).rearrange("p (c r u) -> p c u r", u=2, r=2)
-            return dst, src[:, b0 * P // 2 : b1 * P // 2]
+            src = picked[g][:].bitcast(dtype).rearrange("p (u d b c) -> p b d c u", u=2, d=PIECES, c=GROUP)
+            dst = woven.bitcast(dtype).rearrange("p (b d c u) -> p b d c u", u=2, d=PIECES, c=GROUP)
+            return dst, src[:, b0:b1]
 
         x_mx = {}
 
@@ -140,11 +152,13 @@ def tile_picked_haar_gelu_e_kernel(
         w1_codes = [held([P, H], U32, "w1_codes_%d" % g) for g in range(2)]
         w1_scales = [held([P, H], U8, "w1_scales_%d" % g) for g in range(2)]
 
-        def dealt(grouped):
-            return grouped[:].rearrange("p (t m j) -> p m j t", t=PACK, j=PACK)
-
-        def by_channel(raw):
-            return raw[:].rearrange("p j (m t) -> p m j t", t=PACK)
+        def round_w1(g, raws):
+            grouped = held([P, PACK * H], BF16, "w1_bf%d" % g)
+            dealt = grouped[:].rearrange("p (t m j) -> p m j t", t=PACK, j=PACK)
+            for i, raw in enumerate(raws):
+                by_channel = raw[:].rearrange("p j (m t) -> p m j t", t=PACK)
+                nc.scalar.activation(dealt[:, i * P // 2 : (i + 1) * P // 2], by_channel, ACT.Copy)
+            return grouped
 
         def quantize_w1(g, grouped, t0, t1):
             cols = slice(t0 * P, t1 * P)
@@ -156,20 +170,26 @@ def tile_picked_haar_gelu_e_kernel(
 
         pick(0, 0)
         pick(0, 1)
-        w1_bf0 = held([P, PACK * H], BF16, "w1_bf0")
-        nc.scalar.activation(dealt(w1_bf0), by_channel(w1_raw0), ACT.Copy)
-        halves = (0, EARLY_BANKS)
-        woven0 = [held([P, BANKS // 2 * BAND], BF16, "woven0_%d" % b0) for b0 in halves]
-        scales0 = [two_planes[SCALE_ROWS:, :], held([P, BANKS // 2 * P], U8, "x_scales_0_late")[:]]
-        for woven, b0 in zip(woven0, halves):
-            nc.vector.tensor_copy(*weave_views(woven[:], 0, b0, b0 + BANKS // 2, I32))
-        for woven, scales, b0 in zip(woven0, scales0, halves):
-            quantize_x(held([P, BANKS // 2 * P], U32, "x_codes_0%d" % b0), scales, 0, b0, woven[:])
-        quantize_w1(0, w1_bf0, 0, PACK)
+        quantize_w1(0, round_w1(0, w1_raw0), 0, PACK)
+        late_banks = BANKS - EARLY_BANKS
+        woven_early = held([P, EARLY_BANKS * BAND], BF16, "woven_early")
+        woven_late = placed([P, late_banks * BAND], BF16, "woven_late", W1_PLACES[0])
+        nc.vector.tensor_copy(*weave_views(woven_early[:], 0, 0, EARLY_BANKS, I32))
+        nc.scalar.copy(*weave_views(woven_late[:], 0, EARLY_BANKS, BANKS, U32))
+        early_codes = (
+            (0, held([P, 2 * P], U32, "x_codes_00")),
+            (2, placed([P, P], U32, "x_codes_02", WOVEN_REST_PLACE)),
+            (3, held([P, P], U32, "x_codes_03")),
+        )
+        for b0, codes in early_codes:
+            b1 = b0 + codes.shape[1] // P
+            quantize_x(codes, two_planes[SCALE_ROWS:, b0 * P : b1 * P], 0, b0, woven_early[:, b0 * BAND : b1 * BAND])
+        codes, scales = held([P, late_banks * P], U32, "x_codes_04"), held([P, late_banks * P], U8, "x_scales_04")
+        quantize_x(codes, scales[:], 0, EARLY_BANKS, woven_late[:])
 
-        w1_raw1 = [held([P, PACK, H // 2], F32, "w1_raw1_0"), placed([P, PACK, H // 2], F32, "w1_raw1_1", 0)]
+        w1_raw1 = []
         for i, scales in enumerate((w2_scales, w3_scales)):
-            load_rows(w1_raw1[i], w1, 1, 0, i * H // 2)
+            w1_raw1.append(load_w1_half(1, i))
             load_scales(i, scales, (1,))
         w23_words = [load_words(i, words) for i, words in enumerate((w2_words, w3_words))]
 
@@ -194,19 +214,14 @@ def tile_picked_haar_gelu_e_kernel(
             load_scales(i, scales, (0, 2, 3))
 
         pick(1, 0)
-        pick(1, 1)
+        pick(1, 1, (V + V // 2, S))
         woven_first = held([P, VECTOR_BANKS * BAND], BF16, "woven_first")
         nc.vector.tensor_copy(*weave_views(woven_first[:], 1, 0, VECTOR_BANKS, I32))
 
-        w1_bf1 = held([P, PACK * H], BF16, "w1_bf1")
-        m0 = 0
-        for raw in w1_raw1:
-            m1 = m0 + raw.shape[2] // PACK
-            nc.scalar.activation(dealt(w1_bf1)[:, m0:m1], by_channel(raw), ACT.Copy)
-            m0 = m1
+        w1_bf1 = round_w1(1, w1_raw1)
 
-        first_codes = placed([P, VECTOR_BANKS * P], U32, "x_codes_10", 0)
-        woven_rest = placed([P, (BANKS - VECTOR_BANKS) * BAND], BF16, "woven_rest", 4 * VECTOR_BANKS * P)
+        first_codes = placed([P, VECTOR_BANKS * P], U32, "x_codes_10", W1_PLACES[1])
+        woven_rest = placed([P, (BANKS - VECTOR_BANKS) * BAND], BF16, "woven_rest", WOVEN_REST_PLACE)
         next_banks = BANKS // 2 - VECTOR_BANKS
         woven_next, woven_last = woven_rest[:, : next_banks * BAND], woven_rest[:, next_banks * BAND :]
         nc.scalar.copy(*weave_views(woven_next, 1, VECTOR_BANKS, BANKS // 2, U32))

@@ -33,10 +33,10 @@ X_STEPS = (
     ((1280, 432), (2048, 256)),
     ((1024, 1024), (2048, 0)),
 )
-LAST_FIRST = 896
-LAST_STEPS = ((576, 240), (1152, 192))
-W1_PLACES = (4096, 0)
-WOVEN_REST_PLACE = 8192
+LAST_FIRST = 1024
+LAST_STEPS = ((512, 0), (1024, 160))
+W1_LAST_PLACE = 0
+WOVEN_REST_PLACE = 4096
 VECTOR_BANKS = 2
 
 
@@ -92,11 +92,6 @@ def tile_picked_haar_gelu_e_kernel(
             second = raw[:].rearrange("p (j c) -> p j c", j=2)
             return [(first[:], 0, ((LAST_FIRST, LAST_FIRST),)), (second, LAST_FIRST, LAST_STEPS)]
 
-        def load_w1_half(g, i):
-            shape, name = [P, PACK, H // 2], "w1_raw%d_%d" % (g, i)
-            raw = placed(shape, F32, name, W1_PLACES[g]) if i else held(shape, F32, name)
-            return load_rows(raw, w1, g, 0, i * H // 2)
-
         def load_words(i, words):
             tile = held([P, 2 * N], U8, "w23_words_%d" % i)
             nc.sync.dma_start(out=tile[:].bitcast(I32), in_=words[0].bitcast(I32))
@@ -105,7 +100,7 @@ def tile_picked_haar_gelu_e_kernel(
         x_raw = {(0, 0): load_row_pair(0, 0)}
         nc.sync.dma_start(offsets[:], offs)
         x_raw[0, 1] = load_row_pair(0, 1)
-        w1_raw0 = [load_w1_half(0, i) for i in range(2)]
+        w1_raw0 = [load_rows(held([P, PACK, H], F32, "w1_raw0"), w1, 0, 0, 0)]
         x_raw[1, 0] = load_row_pair(1, 0)
         x_raw[1, 1] = load_last_row_pair()
 
@@ -157,7 +152,8 @@ def tile_picked_haar_gelu_e_kernel(
             dealt = grouped[:].rearrange("p (t m j) -> p m j t", t=PACK, j=PACK)
             for i, raw in enumerate(raws):
                 by_channel = raw[:].rearrange("p j (m t) -> p m j t", t=PACK)
-                nc.scalar.activation(dealt[:, i * P // 2 : (i + 1) * P // 2], by_channel, ACT.Copy)
+                width = P // len(raws)
+                nc.scalar.activation(dealt[:, i * width : (i + 1) * width], by_channel, ACT.Copy)
             return grouped
 
         def quantize_w1(g, grouped, t0, t1):
@@ -170,12 +166,12 @@ def tile_picked_haar_gelu_e_kernel(
 
         pick(0, 0)
         pick(0, 1)
-        quantize_w1(0, round_w1(0, w1_raw0), 0, PACK)
+        w1_bf0 = round_w1(0, w1_raw0)
         late_banks = BANKS - EARLY_BANKS
         woven_early = held([P, EARLY_BANKS * BAND], BF16, "woven_early")
-        woven_late = placed([P, late_banks * BAND], BF16, "woven_late", W1_PLACES[0])
+        woven_late = held([P, late_banks * BAND], BF16, "woven_late")
         nc.vector.tensor_copy(*weave_views(woven_early[:], 0, 0, EARLY_BANKS, I32))
-        nc.scalar.copy(*weave_views(woven_late[:], 0, EARLY_BANKS, BANKS, U32))
+        nc.vector.tensor_copy(*weave_views(woven_late[:], 0, EARLY_BANKS, BANKS, I32))
         early_codes = (
             (0, held([P, 2 * P], U32, "x_codes_00")),
             (2, placed([P, P], U32, "x_codes_02", WOVEN_REST_PLACE)),
@@ -186,10 +182,12 @@ def tile_picked_haar_gelu_e_kernel(
             quantize_x(codes, two_planes[SCALE_ROWS:, b0 * P : b1 * P], 0, b0, woven_early[:, b0 * BAND : b1 * BAND])
         codes, scales = held([P, late_banks * P], U32, "x_codes_04"), held([P, late_banks * P], U8, "x_scales_04")
         quantize_x(codes, scales[:], 0, EARLY_BANKS, woven_late[:])
+        quantize_w1(0, w1_bf0, 0, PACK)
 
-        w1_raw1 = []
+        half = [P, PACK, H // 2]
+        w1_raw1 = [held(half, F32, "w1_raw1_0"), placed(half, F32, "w1_raw1_1", W1_LAST_PLACE)]
         for i, scales in enumerate((w2_scales, w3_scales)):
-            w1_raw1.append(load_w1_half(1, i))
+            load_rows(w1_raw1[i], w1, 1, 0, i * H // 2)
             load_scales(i, scales, (1,))
         w23_words = [load_words(i, words) for i, words in enumerate((w2_words, w3_words))]
 
@@ -220,7 +218,7 @@ def tile_picked_haar_gelu_e_kernel(
 
         w1_bf1 = round_w1(1, w1_raw1)
 
-        first_codes = placed([P, VECTOR_BANKS * P], U32, "x_codes_10", W1_PLACES[1])
+        first_codes = placed([P, VECTOR_BANKS * P], U32, "x_codes_10", W1_LAST_PLACE)
         woven_rest = placed([P, (BANKS - VECTOR_BANKS) * BAND], BF16, "woven_rest", WOVEN_REST_PLACE)
         next_banks = BANKS // 2 - VECTOR_BANKS
         woven_next, woven_last = woven_rest[:, : next_banks * BAND], woven_rest[:, next_banks * BAND :]

@@ -25,19 +25,12 @@ SCALE_ROWS = 4
 RUN = 4
 GROUP = 64
 BANKS = 8
-EARLY_BANKS = 2 * N // P
 SLICE = 128
 BAND = SLICE * PACK
-X_STEPS = (
-    ((1280, 432), (2048, 256)),
-    ((1280, 432), (2048, 256)),
-    ((1024, 1024), (2048, 0)),
-)
-LAST_FIRST = 1024
-LAST_STEPS = ((512, 0), (1024, 160))
-W1_LAST_PLACE = 0
-WOVEN_REST_PLACE = 4096
-VECTOR_BANKS = 2
+EARLY_BANKS = 3
+W1_SCALAR0 = 56
+SCALAR_ENTRIES = 640
+W1_SCALAR = 44
 
 
 def tile_picked_haar_gelu_e_kernel(
@@ -57,139 +50,131 @@ def tile_picked_haar_gelu_e_kernel(
 
         offsets = keep.tile([P, S // LIST_ROWS], U16, name="offsets")
 
-        two_planes = held([P, 2 * N], U8, "two_planes")
-        nc.vector.memset(two_planes[:].bitcast(I32), 0)
-        w23_scales = [two_planes[:, :N], two_planes[:, N:]]
+        w23_plane = held([P, 2 * N], U8, "w23_plane")
+        nc.vector.memset(w23_plane[:].bitcast(I32), 0)
+        w23_scales = [w23_plane[:, :N], w23_plane[:, N:]]
 
         table_warm = held([P, 2], F32, "table_warm")
         nc.vector.memset(table_warm[:, :1], 0.0)
         nc.scalar.activation(table_warm[:, 1:], table_warm[:, :1], ACT.Gelu_apprx_tanh)
 
-        def load_rows(raw, src, g, j0, c0):
-            rows = src[g * K_PASS : (g + 1) * K_PASS, :].rearrange("(p j) c -> p j c", j=PACK)
-            nc.sync.dma_start(out=raw[:], in_=rows[:, j0 : j0 + raw.shape[1], c0 : c0 + raw.shape[2]])
-            return raw
+        w1_raw = [placed([P, PACK * H], F32, "w1_raw0", 8192), placed([P, PACK * H], F32, "w1_raw1", 0)]
 
-        def load_row_pair(g, u):
-            raw = held([P, 2 * T], F32, "x_raw_%d%d" % (g, u))
-            run = xT[g * K_PASS : (g + 1) * K_PASS, :].rearrange("(p j) c -> p (j c)", j=PACK)
-            done = 0
-            for c1, on_scalar in X_STEPS[2 * g + u]:
-                nc.sync.dma_start(out=raw[:, done : T + c1], in_=run[:, 2 * T * u + done : 2 * T * u + T + c1])
-                done = T + c1
-            return [(raw[:].rearrange("p (j c) -> p j c", j=2), 0, X_STEPS[2 * g + u])]
+        def load_w1(g):
+            nc.sync.dma_start(
+                out=w1_raw[g][:], in_=w1[g * K_PASS : (g + 1) * K_PASS, :].rearrange("(p j) c -> p (j c)", j=PACK)
+            )
 
-        def load_last_row_pair():
-            rest = T - LAST_FIRST
-            first = load_rows(held([P, 2, LAST_FIRST], F32, "x_raw_11_first"), xT, 1, 2, 0)
-            raw = held([P, 2 * rest], F32, "x_raw_11_second")
-            rows = xT[K_PASS:, LAST_FIRST:].rearrange("(p j) c -> p j c", j=PACK)
-            nc.sync.dma_start(out=raw[:, :rest], in_=rows[:, 2])
-            done = 0
-            for c1, on_scalar in LAST_STEPS:
-                nc.sync.dma_start(out=raw[:, rest + done : rest + c1], in_=rows[:, 3, done:c1])
-                done = c1
-            second = raw[:].rearrange("p (j c) -> p j c", j=2)
-            return [(first[:], 0, ((LAST_FIRST, LAST_FIRST),)), (second, LAST_FIRST, LAST_STEPS)]
-
-        def load_words(i, words):
+        x_raw = {}
+        for g in range(2):
+            rows = xT[g * K_PASS : (g + 1) * K_PASS, :].rearrange("(p j) c -> p j c", j=PACK)
+            for j in range(PACK):
+                x_raw[g, j] = held([P, T], F32, "x_raw_%d%d" % (g, j))
+                nc.sync.dma_start(out=x_raw[g, j][:], in_=rows[:, j])
+                if (g, j) == (0, 0):
+                    nc.sync.dma_start(offsets[:], offs)
+        load_w1(0)
+        load_w1(1)
+        w23_words = []
+        for i, words in enumerate((w2_words, w3_words)):
             tile = held([P, 2 * N], U8, "w23_words_%d" % i)
             nc.sync.dma_start(out=tile[:].bitcast(I32), in_=words[0].bitcast(I32))
-            return tile
-
-        x_raw = {(0, 0): load_row_pair(0, 0)}
-        nc.sync.dma_start(offsets[:], offs)
-        x_raw[0, 1] = load_row_pair(0, 1)
-        w1_raw0 = [load_rows(held([P, PACK, H], F32, "w1_raw0"), w1, 0, 0, 0)]
-        x_raw[1, 0] = load_row_pair(1, 0)
-        x_raw[1, 1] = load_last_row_pair()
-
-        def load_scales(i, scales, groups):
-            for q in groups:
+            w23_words.append(tile)
+        for i, scales in enumerate((w2_scales, w3_scales)):
+            for q in range(4):
                 nc.sync.dma_start(
                     out=w23_scales[i][32 * q : 32 * q + SCALE_ROWS, :].bitcast(I32),
                     in_=scales[0, SCALE_ROWS * q : SCALE_ROWS * (q + 1), :].bitcast(I32),
                 )
 
-        picked = [held([P, 2 * S], U32, "picked_%d" % g) for g in range(2)]
+        def gather(g, j, e0, e1, on_scalar, dst):
+            window = x_raw[g, j][:].indirect(offsets[:, e0 // LIST_ROWS : e1 // LIST_ROWS])
+            if on_scalar:
+                nc.scalar.activation(dst, window, ACT.Copy)
+            else:
+                nc.vector.tensor_copy(dst, window)
 
-        def pick(g, u, cuts=(S,)):
-            rounded = held([P, 2 * T], BF16, "x_rounded_%d%d" % (g, u))
-            dst = rounded[:].rearrange("p (c r j) -> p c j r", r=RUN, j=2)
-            for raw, base, steps in x_raw[g, u]:
-                src = raw.rearrange("p j (c r) -> p c j r", r=RUN)
-                start = 0
-                for c1, on_scalar in steps:
-                    split, end = start + on_scalar // RUN, c1 // RUN
-                    if split > start:
-                        nc.scalar.activation(dst[:, base // RUN :][:, start:split], src[:, start:split], ACT.Copy)
-                    if split < end:
-                        nc.vector.tensor_copy(out=dst[:, base // RUN :][:, split:end], in_=src[:, split:end])
-                    start = end
-            e0 = 0
-            for e1 in cuts:
-                window = rounded[:].bitcast(U32).indirect(offsets[:, e0 // LIST_ROWS : e1 // LIST_ROWS])
-                nc.vector.tensor_copy(picked[g][:, u * S + e0 : u * S + e1], window)
-                e0 = e1
-
-        def weave_views(woven, g, b0, b1, dtype):
-            src = picked[g][:].bitcast(dtype).rearrange("p (u d b c) -> p b d c u", u=2, d=PIECES, c=GROUP)
-            dst = woven.bitcast(dtype).rearrange("p (b d c u) -> p b d c u", u=2, d=PIECES, c=GROUP)
-            return dst, src[:, b0:b1]
+        def weave(woven, rows, c0, c1, on_scalar=False):
+            src = rows.rearrange("p (j d c r) -> p c d j r", j=PACK, d=PIECES, r=RUN)
+            dst = woven.rearrange("p (c d r j) -> p c d j r", j=PACK, d=PIECES, r=RUN)
+            if on_scalar:
+                nc.scalar.copy(dst, src[:, c0 // RUN : c1 // RUN])
+            else:
+                nc.vector.tensor_copy(out=dst, in_=src[:, c0 // RUN : c1 // RUN])
 
         x_mx = {}
 
-        def quantize_x(codes, scales, g, b0, woven):
-            nc.vector.quantize_mx(out=codes[:].bitcast(FP8X4), scales=scales, in_=woven)
-            for b in range(codes.shape[1] // P):
+        def quantize_x(g, b0, b1, woven, late=False):
+            width = (b1 - b0) * P
+            scales = held([P, width], U8, "x_scales_%d%d" % (g, b0))
+            if late:
+                codes = placed([P, width], U32, "x_codes_%d%d" % (g, b0), b0 * P * 4)
+            else:
+                codes = held([P, width], U32, "x_codes_%d%d" % (g, b0))
+            nc.vector.quantize_mx(out=codes[:].bitcast(FP8X4), scales=scales[:], in_=woven)
+            for b in range(b1 - b0):
                 x_mx[g, b0 + b] = (codes[:, b * P : (b + 1) * P], scales[:, b * P : (b + 1) * P])
 
         w1_codes = [held([P, H], U32, "w1_codes_%d" % g) for g in range(2)]
         w1_scales = [held([P, H], U8, "w1_scales_%d" % g) for g in range(2)]
+        w1_bf = [held([P, PACK * H], BF16, "w1_bf%d" % g) for g in range(2)]
 
-        def round_w1(g, raws):
-            grouped = held([P, PACK * H], BF16, "w1_bf%d" % g)
-            dealt = grouped[:].rearrange("p (t m j) -> p m j t", t=PACK, j=PACK)
-            for i, raw in enumerate(raws):
-                by_channel = raw[:].rearrange("p j (m t) -> p m j t", t=PACK)
-                width = P // len(raws)
-                nc.scalar.activation(dealt[:, i * width : (i + 1) * width], by_channel, ACT.Copy)
-            return grouped
+        def round_w1(g, m0, m1, on_scalar):
+            dealt = w1_bf[g][:].rearrange("p (t m j) -> p m j t", t=PACK, j=PACK)[:, m0:m1]
+            by_channel = w1_raw[g][:].rearrange("p (j m t) -> p m j t", t=PACK, j=PACK)[:, m0:m1]
+            if on_scalar:
+                nc.scalar.activation(dealt, by_channel, ACT.Copy)
+            else:
+                nc.vector.tensor_copy(out=dealt, in_=by_channel)
 
-        def quantize_w1(g, grouped, t0, t1):
+        def quantize_w1(g, t0, t1):
             cols = slice(t0 * P, t1 * P)
             nc.vector.quantize_mx(
                 out=w1_codes[g][:, cols].bitcast(FP8X4),
                 scales=w1_scales[g][:, cols],
-                in_=grouped[:, t0 * P * PACK : t1 * P * PACK],
+                in_=w1_bf[g][:, t0 * P * PACK : t1 * P * PACK],
             )
 
-        pick(0, 0)
-        pick(0, 1)
-        w1_bf0 = round_w1(0, w1_raw0)
-        late_banks = BANKS - EARLY_BANKS
-        woven_early = held([P, EARLY_BANKS * BAND], BF16, "woven_early")
-        woven_late = held([P, late_banks * BAND], BF16, "woven_late")
-        nc.vector.tensor_copy(*weave_views(woven_early[:], 0, 0, EARLY_BANKS, I32))
-        nc.vector.tensor_copy(*weave_views(woven_late[:], 0, EARLY_BANKS, BANKS, I32))
-        early_codes = (
-            (0, held([P, 2 * P], U32, "x_codes_00")),
-            (2, placed([P, P], U32, "x_codes_02", WOVEN_REST_PLACE)),
-            (3, held([P, P], U32, "x_codes_03")),
-        )
-        for b0, codes in early_codes:
-            b1 = b0 + codes.shape[1] // P
-            quantize_x(codes, two_planes[SCALE_ROWS:, b0 * P : b1 * P], 0, b0, woven_early[:, b0 * BAND : b1 * BAND])
-        codes, scales = held([P, late_banks * P], U32, "x_codes_04"), held([P, late_banks * P], U8, "x_scales_04")
-        quantize_x(codes, scales[:], 0, EARLY_BANKS, woven_late[:])
-        quantize_w1(0, w1_bf0, 0, PACK)
-
-        half = [P, PACK, H // 2]
-        w1_raw1 = [held(half, F32, "w1_raw1_0"), placed(half, F32, "w1_raw1_1", W1_LAST_PLACE)]
-        for i, scales in enumerate((w2_scales, w3_scales)):
-            load_rows(w1_raw1[i], w1, 1, 0, i * H // 2)
-            load_scales(i, scales, (1,))
-        w23_words = [load_words(i, words) for i, words in enumerate((w2_words, w3_words))]
+        rows0 = held([P, PACK * S], BF16, "rows0")
+        for j in range(PACK):
+            gather(0, j, 0, SCALAR_ENTRIES, True, rows0[:, j * S : j * S + SCALAR_ENTRIES])
+            gather(0, j, SCALAR_ENTRIES, S, False, rows0[:, j * S + SCALAR_ENTRIES : (j + 1) * S])
+        woven0 = held([P, BANKS * BAND], BF16, "woven0")
+        weave(woven0[:], rows0[:], 0, V)
+        quantize_x(0, 0, BANKS, woven0[:])
+        groups = ((0, 2), (2, 4), (4, 8))
+        rows1 = [held([P, PACK * PIECES * (b1 - b0) * GROUP], BF16, "rows1_%d" % b0) for b0, b1 in groups]
+        for j in range(PACK):
+            for i, (b0, b1) in enumerate(groups):
+                n = (b1 - b0) * GROUP
+                for d in range(PIECES):
+                    on_vector = d == 1 and i != 1
+                    dst = rows1[i][:, (2 * j + d) * n : (2 * j + d + 1) * n]
+                    gather(1, j, d * V + b0 * GROUP, d * V + b1 * GROUP, not on_vector, dst)
+        woven1 = [
+            held([P, 2 * BAND], BF16, "woven1_0"),
+            held([P, 2 * BAND], BF16, "woven1_2"),
+            placed([P, 2 * BAND], BF16, "woven1_4", 8192),
+            placed([P, 2 * BAND], BF16, "woven1_6", 4096),
+        ]
+        weave(woven1[0][:], rows1[0][:], 0, 2 * GROUP)
+        weave(woven1[1][:], rows1[1][:], 0, 2 * GROUP)
+        round_w1(0, 0, W1_SCALAR0, True)
+        round_w1(0, W1_SCALAR0, P, False)
+        quantize_x(1, 0, 2, woven1[0][:])
+        quantize_w1(0, 0, 2)
+        quantize_w1(0, 2, PACK)
+        weave(woven1[2][:, :BAND], rows1[2][:], 0, GROUP)
+        weave(woven1[2][:, BAND:], rows1[2][:], GROUP, 2 * GROUP, True)
+        round_w1(1, 0, W1_SCALAR, True)
+        round_w1(1, W1_SCALAR, P, False)
+        quantize_w1(1, 0, 2)
+        quantize_w1(1, 2, PACK)
+        quantize_x(1, 2, 4, woven1[1][:], True)
+        weave(woven1[3][:, :BAND], rows1[2][:], 2 * GROUP, 3 * GROUP)
+        weave(woven1[3][:, BAND:], rows1[2][:], 3 * GROUP, 4 * GROUP, True)
+        quantize_x(1, 4, 6, woven1[2][:], True)
+        quantize_x(1, 6, 8, woven1[3][:])
 
         banks = [psum.tile([P, PACK, P], F32, name="h_bank_%d" % b, tag="bank%d" % b) for b in range(BANKS)]
 
@@ -208,51 +193,29 @@ def tile_picked_haar_gelu_e_kernel(
         for b in range(EARLY_BANKS):
             for t in range(PACK):
                 first_pass(0, b, t, t == 0, False)
-        for i, scales in enumerate((w2_scales, w3_scales)):
-            load_scales(i, scales, (0, 2, 3))
-
-        pick(1, 0)
-        pick(1, 1, (V + V // 2, S))
-        woven_first = held([P, VECTOR_BANKS * BAND], BF16, "woven_first")
-        nc.vector.tensor_copy(*weave_views(woven_first[:], 1, 0, VECTOR_BANKS, I32))
-
-        w1_bf1 = round_w1(1, w1_raw1)
-
-        first_codes = placed([P, VECTOR_BANKS * P], U32, "x_codes_10", W1_LAST_PLACE)
-        woven_rest = placed([P, (BANKS - VECTOR_BANKS) * BAND], BF16, "woven_rest", WOVEN_REST_PLACE)
-        next_banks = BANKS // 2 - VECTOR_BANKS
-        woven_next, woven_last = woven_rest[:, : next_banks * BAND], woven_rest[:, next_banks * BAND :]
-        nc.scalar.copy(*weave_views(woven_next, 1, VECTOR_BANKS, BANKS // 2, U32))
-        nc.scalar.copy(*weave_views(woven_last, 1, BANKS // 2, BANKS, U32))
-        quantize_w1(1, w1_bf1, 0, PACK // 2)
-        quantize_x(first_codes, held([P, VECTOR_BANKS * P], U8, "x_scales_1_first")[:], 1, 0, woven_first[:])
-        quantize_w1(1, w1_bf1, PACK // 2, PACK)
-        for b0, woven in ((VECTOR_BANKS, woven_next), (BANKS // 2, woven_last)):
-            width = woven.shape[1] // PACK
-            codes, scales = held([P, width], U32, "x_codes_1%d" % b0), held([P, width], U8, "x_scales_1%d" % b0)
-            quantize_x(codes, scales[:], 1, b0, woven)
 
         slices = V // SLICE
-        h = [held([P, 2, PIECES, GROUP * PACK], F32, "h_%d" % s) for s in range(slices)]
+        h = [held([P, 2 * BAND], F32, "h_%d" % s) for s in range(slices)]
         for b in range(BANKS):
             for t in range(PACK):
                 if b < EARLY_BANKS:
                     first_pass(1, b, t, False, t == PACK - 1)
                 else:
-                    first_pass(0, b, t, True, False)
-                    first_pass(1, b, t, False, True)
+                    first_pass(1, b, t, True, False)
+                    first_pass(0, b, t, False, True)
             nc.scalar.activation(
-                h[b // 2][:, b % 2].rearrange("p d (c t) -> p (d c) t", t=PACK),
+                h[b // 2][:, (b % 2) * BAND : (b % 2 + 1) * BAND].rearrange("p (v t) -> p v t", t=PACK),
                 banks[b][:].rearrange("p t v -> p v t"),
                 ACT.Gelu_apprx_tanh,
             )
 
         bands = [held([P, 2 * BAND], BF16, "bands_%d" % s) for s in range(slices)]
 
-        def band(s, i, of_banks=slice(0, 2)):
-            dst = bands[s][:, i * BAND : (i + 1) * BAND].rearrange("p (b x) -> p b x", b=2)
-            op = ALU.add if i == 0 else ALU.subtract
-            nc.vector.tensor_tensor(dst[:, of_banks], h[s][:, of_banks, 0], h[s][:, of_banks, 1], op)
+        def band(s, i, b0=0, b1=2):
+            half = BAND // 2
+            dst = bands[s][:, i * BAND + b0 * half : i * BAND + b1 * half].rearrange("p (c x) -> p c x", x=RUN * PACK)
+            src = h[s][:, b0 * BAND : b1 * BAND].rearrange("p (c d x) -> p d c x", d=PIECES, x=RUN * PACK)
+            nc.vector.tensor_tensor(dst, src[:, 0], src[:, 1], ALU.add if i == 0 else ALU.subtract)
 
         def band_pass(acc, mt, i, codes, scales):
             nc.tensor.matmul_mx(
@@ -299,7 +262,7 @@ def tile_picked_haar_gelu_e_kernel(
 
         for b in range(2):
             for i in range(2):
-                band(0, i, slice(b, b + 1))
+                band(0, i, b, b + 1)
         for s in range(1, slices):
             band(s, 0)
             finish(s - 1)

@@ -27,10 +27,9 @@ GROUP = 64
 BANKS = 8
 SLICE = 128
 BAND = SLICE * PACK
+PAD = 16
 EARLY_BANKS = 3
-W1_SCALAR0 = 56
-SCALAR_ENTRIES = 640
-W1_SCALAR = 44
+W1_SCALAR = (62, 44)
 
 
 def tile_picked_haar_gelu_e_kernel(
@@ -58,23 +57,20 @@ def tile_picked_haar_gelu_e_kernel(
         nc.vector.memset(table_warm[:, :1], 0.0)
         nc.scalar.activation(table_warm[:, 1:], table_warm[:, :1], ACT.Gelu_apprx_tanh)
 
-        w1_raw = [placed([P, PACK * H], F32, "w1_raw0", 8192), placed([P, PACK * H], F32, "w1_raw1", 0)]
-
-        def load_w1(g):
+        window = {}
+        for g, j0, j1 in ((0, 0, 2), (0, 2, 4), (1, 0, 1), (1, 1, 2), (1, 2, 3), (1, 3, 4)):
+            rows = xT[g * K_PASS : (g + 1) * K_PASS, :].rearrange("(p j) c -> p (j c)", j=PACK)
+            raw = held([P, (j1 - j0) * T], F32, "x_raw_%d%d" % (g, j0))
+            nc.sync.dma_start(out=raw[:], in_=rows[:, j0 * T : j1 * T])
+            for j in range(j0, j1):
+                window[g, j] = raw[:, (j - j0) * T : (j - j0 + 1) * T]
+            if (g, j0) == (0, 0):
+                nc.sync.dma_start(offsets[:], offs)
+        w1_raw = [placed([P, PACK * H], F32, "w1_raw%d" % g, g * 8192) for g in range(2)]
+        for g in range(2):
             nc.sync.dma_start(
                 out=w1_raw[g][:], in_=w1[g * K_PASS : (g + 1) * K_PASS, :].rearrange("(p j) c -> p (j c)", j=PACK)
             )
-
-        x_raw = {}
-        for g in range(2):
-            rows = xT[g * K_PASS : (g + 1) * K_PASS, :].rearrange("(p j) c -> p j c", j=PACK)
-            for j in range(PACK):
-                x_raw[g, j] = held([P, T], F32, "x_raw_%d%d" % (g, j))
-                nc.sync.dma_start(out=x_raw[g, j][:], in_=rows[:, j])
-                if (g, j) == (0, 0):
-                    nc.sync.dma_start(offsets[:], offs)
-        load_w1(0)
-        load_w1(1)
         w23_words = []
         for i, words in enumerate((w2_words, w3_words)):
             tile = held([P, 2 * N], U8, "w23_words_%d" % i)
@@ -87,30 +83,43 @@ def tile_picked_haar_gelu_e_kernel(
                     in_=scales[0, SCALE_ROWS * q : SCALE_ROWS * (q + 1), :].bitcast(I32),
                 )
 
-        def gather(g, j, e0, e1, on_scalar, dst):
-            window = x_raw[g, j][:].indirect(offsets[:, e0 // LIST_ROWS : e1 // LIST_ROWS])
-            if on_scalar:
-                nc.scalar.activation(dst, window, ACT.Copy)
-            else:
-                nc.vector.tensor_copy(dst, window)
+        half_v = V // 2
+        span = (V, half_v)
+        picked = {
+            (g, a): held([P, PACK * PIECES * (span[g] + PAD)], F32, "picked_%d%d" % (g, a))
+            for g in range(2)
+            for a in range(V // span[g])
+        }
 
-        def weave(woven, rows, c0, c1, on_scalar=False):
-            src = rows.rearrange("p (j d c r) -> p c d j r", j=PACK, d=PIECES, r=RUN)
+        def gather(g, j, d, v0, v1, on_scalar):
+            a = v0 // span[g]
+            at = (j * PIECES + d) * (span[g] + PAD) - a * span[g]
+            dst = picked[g, a][:, at + v0 : at + v1]
+            src = window[g, j].indirect(offsets[:, (d * V + v0) // LIST_ROWS : (d * V + v1) // LIST_ROWS])
+            if on_scalar:
+                nc.scalar.activation(dst, src, ACT.Copy)
+            else:
+                nc.vector.tensor_copy(dst, src)
+
+        def weave(g, b0, b1, woven, on_scalar=False):
+            a = b0 * GROUP // span[g]
+            src = picked[g, a][:].rearrange("p (j d c r) -> p c d j r", j=PACK, d=PIECES, r=RUN)
+            src = src[:, (b0 * GROUP - a * span[g]) // RUN : (b1 * GROUP - a * span[g]) // RUN]
             dst = woven.rearrange("p (c d r j) -> p c d j r", j=PACK, d=PIECES, r=RUN)
             if on_scalar:
-                nc.scalar.copy(dst, src[:, c0 // RUN : c1 // RUN])
+                nc.scalar.copy(dst, src)
             else:
-                nc.vector.tensor_copy(out=dst, in_=src[:, c0 // RUN : c1 // RUN])
+                nc.vector.tensor_copy(out=dst, in_=src)
 
         x_mx = {}
 
-        def quantize_x(g, b0, b1, woven, late=False):
+        def quantize_x(g, b0, b1, woven, offset=None):
             width = (b1 - b0) * P
             scales = held([P, width], U8, "x_scales_%d%d" % (g, b0))
-            if late:
-                codes = placed([P, width], U32, "x_codes_%d%d" % (g, b0), b0 * P * 4)
-            else:
+            if offset is None:
                 codes = held([P, width], U32, "x_codes_%d%d" % (g, b0))
+            else:
+                codes = placed([P, width], U32, "x_codes_%d%d" % (g, b0), offset)
             nc.vector.quantize_mx(out=codes[:].bitcast(FP8X4), scales=scales[:], in_=woven)
             for b in range(b1 - b0):
                 x_mx[g, b0 + b] = (codes[:, b * P : (b + 1) * P], scales[:, b * P : (b + 1) * P])
@@ -119,13 +128,12 @@ def tile_picked_haar_gelu_e_kernel(
         w1_scales = [held([P, H], U8, "w1_scales_%d" % g) for g in range(2)]
         w1_bf = [held([P, PACK * H], BF16, "w1_bf%d" % g) for g in range(2)]
 
-        def round_w1(g, m0, m1, on_scalar):
-            dealt = w1_bf[g][:].rearrange("p (t m j) -> p m j t", t=PACK, j=PACK)[:, m0:m1]
-            by_channel = w1_raw[g][:].rearrange("p (j m t) -> p m j t", t=PACK, j=PACK)[:, m0:m1]
-            if on_scalar:
-                nc.scalar.activation(dealt, by_channel, ACT.Copy)
-            else:
-                nc.vector.tensor_copy(out=dealt, in_=by_channel)
+        def round_w1(g):
+            dealt = w1_bf[g][:].rearrange("p (t m j) -> p m j t", t=PACK, j=PACK)
+            by_channel = w1_raw[g][:].rearrange("p (j m t) -> p m j t", t=PACK, j=PACK)
+            m = W1_SCALAR[g]
+            nc.scalar.activation(dealt[:, :m], by_channel[:, :m], ACT.Copy)
+            nc.vector.tensor_copy(out=dealt[:, m:], in_=by_channel[:, m:])
 
         def quantize_w1(g, t0, t1):
             cols = slice(t0 * P, t1 * P)
@@ -135,45 +143,43 @@ def tile_picked_haar_gelu_e_kernel(
                 in_=w1_bf[g][:, t0 * P * PACK : t1 * P * PACK],
             )
 
-        rows0 = held([P, PACK * S], BF16, "rows0")
         for j in range(PACK):
-            gather(0, j, 0, SCALAR_ENTRIES, True, rows0[:, j * S : j * S + SCALAR_ENTRIES])
-            gather(0, j, SCALAR_ENTRIES, S, False, rows0[:, j * S + SCALAR_ENTRIES : (j + 1) * S])
+            for d in range(PIECES):
+                gather(0, j, d, 0, V, d == 0)
         woven0 = held([P, BANKS * BAND], BF16, "woven0")
-        weave(woven0[:], rows0[:], 0, V)
+        weave(0, 0, BANKS, woven0[:])
         quantize_x(0, 0, BANKS, woven0[:])
-        groups = ((0, 2), (2, 4), (4, 8))
-        rows1 = [held([P, PACK * PIECES * (b1 - b0) * GROUP], BF16, "rows1_%d" % b0) for b0, b1 in groups]
-        for j in range(PACK):
-            for i, (b0, b1) in enumerate(groups):
-                n = (b1 - b0) * GROUP
+        for j in range(PACK - 1):
+            for a in range(2):
                 for d in range(PIECES):
-                    on_vector = d == 1 and i != 1
-                    dst = rows1[i][:, (2 * j + d) * n : (2 * j + d + 1) * n]
-                    gather(1, j, d * V + b0 * GROUP, d * V + b1 * GROUP, not on_vector, dst)
+                    gather(1, j, d, a * half_v, (a + 1) * half_v, not (d == 1 and (j == 2 or (j, a) == (1, 1))))
+        last = PACK - 1
+        gather(1, last, 0, 0, 128, True)
+        gather(1, last, 1, 0, 128, False)
+        gather(1, last, 0, 128, 256, True)
+        gather(1, last, 1, 128, 256, False)
+        gather(1, last, 0, 256, 512, True)
+        gather(1, last, 1, 256, 512, True)
         woven1 = [
             held([P, 2 * BAND], BF16, "woven1_0"),
-            held([P, 2 * BAND], BF16, "woven1_2"),
-            placed([P, 2 * BAND], BF16, "woven1_4", 8192),
-            placed([P, 2 * BAND], BF16, "woven1_6", 4096),
+            held([P, 3 * BAND], BF16, "woven1_2"),
+            placed([P, BAND], BF16, "woven1_5", 0),
+            placed([P, 2 * BAND], BF16, "woven1_6", 8192),
         ]
-        weave(woven1[0][:], rows1[0][:], 0, 2 * GROUP)
-        weave(woven1[1][:], rows1[1][:], 0, 2 * GROUP)
-        round_w1(0, 0, W1_SCALAR0, True)
-        round_w1(0, W1_SCALAR0, P, False)
+        weave(1, 0, 2, woven1[0][:])
+        weave(1, 2, 4, woven1[1][:, : 2 * BAND])
         quantize_x(1, 0, 2, woven1[0][:])
+        weave(1, 4, 5, woven1[1][:, 2 * BAND :])
+        round_w1(0)
+        weave(1, 5, 6, woven1[2][:], True)
         quantize_w1(0, 0, 2)
         quantize_w1(0, 2, PACK)
-        weave(woven1[2][:, :BAND], rows1[2][:], 0, GROUP)
-        weave(woven1[2][:, BAND:], rows1[2][:], GROUP, 2 * GROUP, True)
-        round_w1(1, 0, W1_SCALAR, True)
-        round_w1(1, W1_SCALAR, P, False)
-        quantize_w1(1, 0, 2)
-        quantize_w1(1, 2, PACK)
-        quantize_x(1, 2, 4, woven1[1][:], True)
-        weave(woven1[3][:, :BAND], rows1[2][:], 2 * GROUP, 3 * GROUP)
-        weave(woven1[3][:, BAND:], rows1[2][:], 3 * GROUP, 4 * GROUP, True)
-        quantize_x(1, 4, 6, woven1[2][:], True)
+        round_w1(1)
+        quantize_w1(1, 0, 3)
+        quantize_w1(1, 3, PACK)
+        weave(1, 6, 8, woven1[3][:], True)
+        quantize_x(1, 2, 5, woven1[1][:], 8192 + 4096)
+        quantize_x(1, 5, 6, woven1[2][:], 8192 + 6144)
         quantize_x(1, 6, 8, woven1[3][:])
 
         banks = [psum.tile([P, PACK, P], F32, name="h_bank_%d" % b, tag="bank%d" % b) for b in range(BANKS)]
@@ -194,8 +200,15 @@ def tile_picked_haar_gelu_e_kernel(
             for t in range(PACK):
                 first_pass(0, b, t, t == 0, False)
 
-        slices = V // SLICE
-        h = [held([P, 2 * BAND], F32, "h_%d" % s) for s in range(slices)]
+        h = [held([P, BAND], F32, "h_%d" % b) for b in range(BANKS)]
+
+        def gelu(b, c0, c1):
+            nc.scalar.activation(
+                h[b][:, c0 * PACK : c1 * PACK].rearrange("p (v t) -> p v t", t=PACK),
+                banks[b][:, :, c0:c1].rearrange("p t v -> p v t"),
+                ACT.Gelu_apprx_tanh,
+            )
+
         for b in range(BANKS):
             for t in range(PACK):
                 if b < EARLY_BANKS:
@@ -203,18 +216,19 @@ def tile_picked_haar_gelu_e_kernel(
                 else:
                     first_pass(1, b, t, True, False)
                     first_pass(0, b, t, False, True)
-            nc.scalar.activation(
-                h[b // 2][:, (b % 2) * BAND : (b % 2 + 1) * BAND].rearrange("p (v t) -> p v t", t=PACK),
-                banks[b][:].rearrange("p t v -> p v t"),
-                ACT.Gelu_apprx_tanh,
-            )
+            if b == 0:
+                gelu(b, 0, P // 2)
+                gelu(b, P // 2, P)
+            else:
+                gelu(b, 0, P)
 
+        slices = V // SLICE
         bands = [held([P, 2 * BAND], BF16, "bands_%d" % s) for s in range(slices)]
 
-        def band(s, i, b0=0, b1=2):
-            half = BAND // 2
-            dst = bands[s][:, i * BAND + b0 * half : i * BAND + b1 * half].rearrange("p (c x) -> p c x", x=RUN * PACK)
-            src = h[s][:, b0 * BAND : b1 * BAND].rearrange("p (c d x) -> p d c x", d=PIECES, x=RUN * PACK)
+        def band(b, i, c0=0, c1=P):
+            at = i * BAND + (b % 2) * (BAND // 2)
+            dst = bands[b // 2][:, at + c0 * 2 : at + c1 * 2].rearrange("p (c x) -> p c x", x=RUN * PACK)
+            src = h[b][:, c0 * PACK : c1 * PACK].rearrange("p (c d x) -> p d c x", d=PIECES, x=RUN * PACK)
             nc.vector.tensor_tensor(dst, src[:, 0], src[:, 1], ALU.add if i == 0 else ALU.subtract)
 
         def band_pass(acc, mt, i, codes, scales):
@@ -228,19 +242,20 @@ def tile_picked_haar_gelu_e_kernel(
                 stop=(i == 1),
             )
 
-        def finish(s):
+        def product(s, acc):
             codes = held([P, 2 * SLICE], U32, "band_codes_%d" % s)
             scales = held([P, 2 * SLICE], U8, "band_scales_%d" % s)
             nc.vector.quantize_mx(out=codes[:].bitcast(FP8X4), scales=scales[:], in_=bands[s][:])
-            acc = psum.tile([P, 2, SLICE], F32, name="acc_%d" % s, tag="bank%d" % (BANKS - slices + 1 + s))
             for mt in range(N // P):
                 for i in range(2):
                     cols = slice(i * SLICE, (i + 1) * SLICE)
                     band_pass(acc[:, mt, :], mt, i, codes[:, cols], scales[:, cols])
-            result = held([P, 2, SLICE], F32, "result_%d" % s)
-            nc.scalar.activation(result[:], acc[:], ACT.Copy, scale=0.5)
+
+        def store(acc, s0, s1):
+            result = held([P, 2, (s1 - s0) * SLICE], F32, "result_%d" % s0)
+            nc.scalar.activation(result[:], acc, ACT.Copy, scale=0.5)
             nc.sync.dma_start(
-                out=out[:, s * SLICE : (s + 1) * SLICE].rearrange("(mt p) v -> p mt v", p=P), in_=result[:]
+                out=out[:, s0 * SLICE : s1 * SLICE].rearrange("(mt p) v -> p mt v", p=P), in_=result[:]
             )
 
         def finish_last(s):
@@ -260,11 +275,20 @@ def tile_picked_haar_gelu_e_kernel(
             nc.scalar.activation(results[1][:], accs[1][:], ACT.Copy, scale=0.5)
             nc.scalar.dma_start(out=out[P:, cols], in_=results[1][:])
 
-        for b in range(2):
+        acc01 = psum.tile([P, 2, 2 * SLICE], F32, name="acc01", tag="bank7")
+        acc2 = psum.tile([P, 2, SLICE], F32, name="acc2", tag="bank6")
+        for c0 in (0, P // 2):
             for i in range(2):
-                band(0, i, b, b + 1)
-        for s in range(1, slices):
-            band(s, 0)
-            finish(s - 1)
-            band(s, 1)
+                band(0, i, c0, c0 + P // 2)
+        for b in range(1, BANKS):
+            band(b, 0)
+            if b == 2:
+                product(0, acc01[:, :, :SLICE])
+            if b == 4:
+                product(1, acc01[:, :, SLICE:])
+                store(acc01[:], 0, 2)
+            if b == 6:
+                product(2, acc2[:])
+                store(acc2[:], 2, 3)
+            band(b, 1)
         finish_last(slices - 1)

@@ -27,7 +27,7 @@ GROUP = 64
 BANKS = 8
 SLICE = 128
 BAND = SLICE * PACK
-PAD = 16
+PAD = 0
 EARLY_BANKS = 3
 W1_SCALAR = (62, 44)
 

@@ -29,7 +29,7 @@ SLICE = 128
 BAND = SLICE * PACK
 PAD = 0
 EARLY_BANKS = 3
-W1_SCALAR = (62, 44)
+W1_SCALAR = (30, 22)
 
 
 def tile_picked_haar_gelu_e_kernel(
@@ -129,10 +129,10 @@ def tile_picked_haar_gelu_e_kernel(
         w1_bf = [held([P, PACK * H], BF16, "w1_bf%d" % g) for g in range(2)]
 
         def round_w1(g):
-            dealt = w1_bf[g][:].rearrange("p (t m j) -> p m j t", t=PACK, j=PACK)
-            by_channel = w1_raw[g][:].rearrange("p (j m t) -> p m j t", t=PACK, j=PACK)
+            dealt = w1_bf[g][:].rearrange("p (t m e j) -> p m j e t", t=PACK, e=2, j=PACK)
+            by_channel = w1_raw[g][:].rearrange("p (j m e t) -> p m j e t", t=PACK, e=2, j=PACK)
             m = W1_SCALAR[g]
-            nc.scalar.activation(dealt[:, :m], by_channel[:, :m], ACT.Copy)
+            nc.scalar.copy(dealt[:, :m], by_channel[:, :m])
             nc.vector.tensor_copy(out=dealt[:, m:], in_=by_channel[:, m:])
 
         def quantize_w1(g, t0, t1):

@@ -29,6 +29,7 @@ SLICE = 128
 BAND = SLICE * PACK
 PAD = 0
 EARLY_BANKS = 3
+WARM_PASSES = 4
 W1_SCALAR = (30, 22)
 
 
@@ -121,6 +122,7 @@ def tile_picked_haar_gelu_e_kernel(
             else:
                 codes = placed([P, width], U32, "x_codes_%d%d" % (g, b0), offset)
             nc.vector.quantize_mx(out=codes[:].bitcast(FP8X4), scales=scales[:], in_=woven)
+            x_mx[g, b0, b1] = (codes, scales)
             for b in range(b1 - b0):
                 x_mx[g, b0 + b] = (codes[:, b * P : (b + 1) * P], scales[:, b * P : (b + 1) * P])
 
@@ -181,6 +183,18 @@ def tile_picked_haar_gelu_e_kernel(
         quantize_x(1, 2, 5, woven1[1][:], 8192 + 4096)
         quantize_x(1, 5, 6, woven1[2][:], 8192 + 6144)
         quantize_x(1, 6, 8, woven1[3][:])
+
+        unread = psum.tile([P, 2 * P], F32, name="unread", tag="bank%d" % (BANKS - 1))
+        for n in range(WARM_PASSES):
+            nc.tensor.matmul_mx(
+                out=unread[:],
+                lhsT=x_mx[1, 0][0].bitcast(FP8X4),
+                lhsT_scale=x_mx[1, 0][1],
+                rhs=x_mx[1, 0, 2][0][:].bitcast(FP8X4),
+                rhs_scale=x_mx[1, 0, 2][1][:],
+                start=True,
+                stop=True,
+            )
 
         banks = [psum.tile([P, PACK, P], F32, name="h_bank_%d" % b, tag="bank%d" % b) for b in range(BANKS)]
 

@@ -30,7 +30,8 @@ BAND = SLICE * PACK
 PAD = 0
 EARLY_BANKS = 3
 WARM_PASSES = 4
-W1_SCALAR = (30, 22)
+FIRST_CUTS = ((0, 64), (64, 128))
+W1_SCALAR = (28, 50)
 
 
 def tile_picked_haar_gelu_e_kernel(
@@ -59,7 +60,7 @@ def tile_picked_haar_gelu_e_kernel(
         nc.scalar.activation(table_warm[:, 1:], table_warm[:, :1], ACT.Gelu_apprx_tanh)
 
         window = {}
-        for g, j0, j1 in ((0, 0, 2), (0, 2, 4), (1, 0, 1), (1, 1, 2), (1, 2, 3), (1, 3, 4)):
+        for g, j0, j1 in ((0, 0, 1), (0, 1, 2), (0, 2, 3), (0, 3, 4), (1, 0, 1), (1, 1, 2), (1, 2, 3), (1, 3, 4)):
             rows = xT[g * K_PASS : (g + 1) * K_PASS, :].rearrange("(p j) c -> p (j c)", j=PACK)
             raw = held([P, (j1 - j0) * T], F32, "x_raw_%d%d" % (g, j0))
             nc.sync.dma_start(out=raw[:], in_=rows[:, j0 * T : j1 * T])
@@ -102,11 +103,12 @@ def tile_picked_haar_gelu_e_kernel(
             else:
                 nc.vector.tensor_copy(dst, src)
 
-        def weave(g, b0, b1, woven, on_scalar=False):
+        def weave(g, b0, b1, woven, on_scalar=False, j0=0, j1=PACK):
             a = b0 * GROUP // span[g]
             src = picked[g, a][:].rearrange("p (j d c r) -> p c d j r", j=PACK, d=PIECES, r=RUN)
             src = src[:, (b0 * GROUP - a * span[g]) // RUN : (b1 * GROUP - a * span[g]) // RUN]
             dst = woven.rearrange("p (c d r j) -> p c d j r", j=PACK, d=PIECES, r=RUN)
+            src, dst = src[:, :, :, j0:j1], dst[:, :, :, j0:j1]
             if on_scalar:
                 nc.scalar.copy(dst, src)
             else:
@@ -137,6 +139,14 @@ def tile_picked_haar_gelu_e_kernel(
             nc.scalar.copy(dealt[:, :m], by_channel[:, :m])
             nc.vector.tensor_copy(out=dealt[:, m:], in_=by_channel[:, m:])
 
+        def round_last():
+            dealt = w1_bf[1][:].rearrange("p (t m e j) -> p m j e t", t=PACK, e=2, j=PACK)
+            by_channel = w1_raw[1][:].rearrange("p (j m e t) -> p m j e t", t=PACK, e=2, j=PACK)
+            m = W1_SCALAR[1]
+            nc.vector.tensor_copy(out=dealt[:, :, :, :, :2], in_=by_channel[:, :, :, :, :2])
+            nc.scalar.copy(dealt[:, :m, :, :, 2:], by_channel[:, :m, :, :, 2:])
+            nc.vector.tensor_copy(out=dealt[:, m:, :, :, 2:], in_=by_channel[:, m:, :, :, 2:])
+
         def quantize_w1(g, t0, t1):
             cols = slice(t0 * P, t1 * P)
             nc.vector.quantize_mx(
@@ -154,8 +164,10 @@ def tile_picked_haar_gelu_e_kernel(
         for j in range(PACK - 1):
             for a in range(2):
                 for d in range(PIECES):
-                    gather(1, j, d, a * half_v, (a + 1) * half_v, not (d == 1 and (j == 2 or (j, a) == (1, 1))))
+                    gather(1, j, d, a * half_v, (a + 1) * half_v, (j, a, d) not in ((1, 0, 1), (1, 1, 1), (2, 0, 1)))
         last = PACK - 1
+        ahead = held([P, 4 * BAND], BF16, "woven_ahead")
+        weave(1, 0, 4, ahead[:], False, 0, last)
         gather(1, last, 0, 0, 128, True)
         gather(1, last, 1, 0, 128, False)
         gather(1, last, 0, 128, 256, True)
@@ -163,35 +175,34 @@ def tile_picked_haar_gelu_e_kernel(
         gather(1, last, 0, 256, 512, True)
         gather(1, last, 1, 256, 512, True)
         woven1 = [
-            held([P, 2 * BAND], BF16, "woven1_0"),
-            held([P, 3 * BAND], BF16, "woven1_2"),
-            placed([P, BAND], BF16, "woven1_5", 0),
+            placed([P, 2 * BAND], BF16, "woven1_4", 0),
             placed([P, 2 * BAND], BF16, "woven1_6", 8192),
         ]
-        weave(1, 0, 2, woven1[0][:])
-        weave(1, 2, 4, woven1[1][:, : 2 * BAND])
-        quantize_x(1, 0, 2, woven1[0][:])
-        weave(1, 4, 5, woven1[1][:, 2 * BAND :])
+        weave(1, 0, 2, ahead[:, : 2 * BAND], False, last, PACK)
+        weave(1, 2, 4, ahead[:, 2 * BAND :], False, last, PACK)
+        quantize_x(1, 0, 2, ahead[:, : 2 * BAND])
+        quantize_x(1, 2, 4, ahead[:, 2 * BAND :])
         round_w1(0)
-        weave(1, 5, 6, woven1[2][:], True)
+        weave(1, 4, 5, woven1[0][:, :BAND])
+        weave(1, 5, 6, woven1[0][:, BAND:], True)
         quantize_w1(0, 0, 2)
         quantize_w1(0, 2, PACK)
-        round_w1(1)
-        quantize_w1(1, 0, 3)
-        quantize_w1(1, 3, PACK)
-        weave(1, 6, 8, woven1[3][:], True)
-        quantize_x(1, 2, 5, woven1[1][:], 8192 + 4096)
-        quantize_x(1, 5, 6, woven1[2][:], 8192 + 6144)
-        quantize_x(1, 6, 8, woven1[3][:])
+        round_last()
+        quantize_w1(1, 0, 2)
+        quantize_w1(1, 2, PACK)
+        weave(1, 6, 7, woven1[1][:, :BAND], True)
+        quantize_x(1, 4, 6, woven1[0][:], 8192 + 4096)
+        weave(1, 7, 8, woven1[1][:, BAND:])
+        quantize_x(1, 6, 8, woven1[1][:])
 
         unread = psum.tile([P, 2 * P], F32, name="unread", tag="bank%d" % (BANKS - 1))
         for n in range(WARM_PASSES):
             nc.tensor.matmul_mx(
                 out=unread[:],
-                lhsT=x_mx[1, 0][0].bitcast(FP8X4),
-                lhsT_scale=x_mx[1, 0][1],
-                rhs=x_mx[1, 0, 2][0][:].bitcast(FP8X4),
-                rhs_scale=x_mx[1, 0, 2][1][:],
+                lhsT=x_mx[1, 2][0].bitcast(FP8X4),
+                lhsT_scale=x_mx[1, 2][1],
+                rhs=x_mx[1, 2, 4][0][:].bitcast(FP8X4),
+                rhs_scale=x_mx[1, 2, 4][1][:],
                 start=True,
                 stop=True,
             )
@@ -230,9 +241,9 @@ def tile_picked_haar_gelu_e_kernel(
                 else:
                     first_pass(1, b, t, True, False)
                     first_pass(0, b, t, False, True)
-            if b == 0:
-                gelu(b, 0, P // 2)
-                gelu(b, P // 2, P)
+            if b < 2:
+                for c0, c1 in FIRST_CUTS:
+                    gelu(b, c0, c1)
             else:
                 gelu(b, 0, P)
 
@@ -291,10 +302,11 @@ def tile_picked_haar_gelu_e_kernel(
 
         acc01 = psum.tile([P, 2, 2 * SLICE], F32, name="acc01", tag="bank7")
         acc2 = psum.tile([P, 2, SLICE], F32, name="acc2", tag="bank6")
-        for c0 in (0, P // 2):
-            for i in range(2):
-                band(0, i, c0, c0 + P // 2)
-        for b in range(1, BANKS):
+        for b in range(2):
+            for c0, c1 in FIRST_CUTS:
+                for i in range(2):
+                    band(b, i, c0, c1)
+        for b in range(2, BANKS):
             band(b, 0)
             if b == 2:
                 product(0, acc01[:, :, :SLICE])

from contextlib import ExitStack

import concourse.mybir as mybir

K, T, S, V, H, N = 1024, 2048, 1024, 512, 512, 256
FLOPS = 2 * K * H * S + 2 * 2 * H * N * V

F32 = mybir.dt.float32
BF16 = mybir.dt.bfloat16
I32 = mybir.dt.int32
U32 = mybir.dt.uint32
U16 = mybir.dt.uint16
U8 = mybir.dt.uint8
FP8X4 = mybir.dt.float8_e4m3fn_x4
FP4X4 = mybir.dt.float4_e2m1fn_x4
ACT = mybir.ActivationFunctionType
ALU = mybir.AluOpType

P = 128
PACK = 4
K_PASS = P * PACK
PIECES = 2
LIST_ROWS = 16
SCALE_ROWS = 4
RUN = 4
GROUP = 64
BANKS = 8
SLICE = 128
BAND = SLICE * PACK
PAD = 0
EARLY_BANKS = 3
WARM_PASSES = 4
FIRST_CUTS = ((0, 64), (64, 128))
W1_SCALAR = (28, 50)


def tile_picked_haar_gelu_e_kernel(
    tc, xT, w1, w2_words, w2_scales, w3_words, w3_scales, offs, out
):
    nc = tc.nc
    with ExitStack() as ctx:
        keep = ctx.enter_context(tc.tile_pool(name="keep", bufs=1))
        shared = ctx.enter_context(tc.tile_pool(name="shared", bufs=1))
        psum = ctx.enter_context(tc.psum_pool(name="psum", bufs=1))

        def held(shape, dtype, name):
            return keep.tile(shape, dtype, name=name, align_bytes=256)

        def placed(shape, dtype, name, offset):
            return shared.tile(shape, dtype, name=name, offset=offset, align_bytes=256)

        offsets = keep.tile([P, S // LIST_ROWS], U16, name="offsets")

        w23_plane = held([P, 2 * N], U8, "w23_plane")
        nc.vector.memset(w23_plane[:].bitcast(I32), 0)
        w23_scales = [w23_plane[:, :N], w23_plane[:, N:]]

        table_warm = held([P, 2], F32, "table_warm")
        nc.vector.memset(table_warm[:, :1], 0.0)
        nc.scalar.activation(table_warm[:, 1:], table_warm[:, :1], ACT.Gelu_apprx_tanh)

        window = {}
        for g, j0, j1 in ((0, 0, 1), (0, 1, 2), (0, 2, 3), (0, 3, 4), (1, 0, 1), (1, 1, 2), (1, 2, 3), (1, 3, 4)):
            rows = xT[g * K_PASS : (g + 1) * K_PASS, :].rearrange("(p j) c -> p (j c)", j=PACK)
            raw = held([P, (j1 - j0) * T], F32, "x_raw_%d%d" % (g, j0))
            nc.sync.dma_start(out=raw[:], in_=rows[:, j0 * T : j1 * T])
            for j in range(j0, j1):
                window[g, j] = raw[:, (j - j0) * T : (j - j0 + 1) * T]
            if (g, j0) == (0, 0):
                nc.sync.dma_start(offsets[:], offs)
        w1_raw = [placed([P, PACK * H], F32, "w1_raw%d" % g, g * 8192) for g in range(2)]
        for g in range(2):
            nc.sync.dma_start(
                out=w1_raw[g][:], in_=w1[g * K_PASS : (g + 1) * K_PASS, :].rearrange("(p j) c -> p (j c)", j=PACK)
            )
        w23_words = []
        for i, words in enumerate((w2_words, w3_words)):
            tile = held([P, 2 * N], U8, "w23_words_%d" % i)
            nc.sync.dma_start(out=tile[:].bitcast(I32), in_=words[0].bitcast(I32))
            w23_words.append(tile)
        for i, scales in enumerate((w2_scales, w3_scales)):
            for q in range(4):
                nc.sync.dma_start(
                    out=w23_scales[i][32 * q : 32 * q + SCALE_ROWS, :].bitcast(I32),
                    in_=scales[0, SCALE_ROWS * q : SCALE_ROWS * (q + 1), :].bitcast(I32),
                )

        half_v = V // 2
        span = (V, half_v)
        picked = {
            (g, a): held([P, PACK * PIECES * (span[g] + PAD)], F32, "picked_%d%d" % (g, a))
            for g in range(2)
            for a in range(V // span[g])
        }

        def gather(g, j, d, v0, v1, on_scalar):
            a = v0 // span[g]
            at = (j * PIECES + d) * (span[g] + PAD) - a * span[g]
            dst = picked[g, a][:, at + v0 : at + v1]
            src = window[g, j].indirect(offsets[:, (d * V + v0) // LIST_ROWS : (d * V + v1) // LIST_ROWS])
            if on_scalar:
                nc.scalar.activation(dst, src, ACT.Copy)
            else:
                nc.vector.tensor_copy(dst, src)

        def weave(g, b0, b1, woven, on_scalar=False, j0=0, j1=PACK):
            a = b0 * GROUP // span[g]
            src = picked[g, a][:].rearrange("p (j d c r) -> p c d j r", j=PACK, d=PIECES, r=RUN)
            src = src[:, (b0 * GROUP - a * span[g]) // RUN : (b1 * GROUP - a * span[g]) // RUN]
            dst = woven.rearrange("p (c d r j) -> p c d j r", j=PACK, d=PIECES, r=RUN)
            src, dst = src[:, :, :, j0:j1], dst[:, :, :, j0:j1]
            if on_scalar:
                nc.scalar.copy(dst, src)
            else:
                nc.vector.tensor_copy(out=dst, in_=src)

        x_mx = {}

        def quantize_x(g, b0, b1, woven, offset=None):
            width = (b1 - b0) * P
            scales = held([P, width], U8, "x_scales_%d%d" % (g, b0))
            if offset is None:
                codes = held([P, width], U32, "x_codes_%d%d" % (g, b0))
            else:
                codes = placed([P, width], U32, "x_codes_%d%d" % (g, b0), offset)
            nc.vector.quantize_mx(out=codes[:].bitcast(FP8X4), scales=scales[:], in_=woven)
            x_mx[g, b0, b1] = (codes, scales)
            for b in range(b1 - b0):
                x_mx[g, b0 + b] = (codes[:, b * P : (b + 1) * P], scales[:, b * P : (b + 1) * P])

        w1_codes = [held([P, H], U32, "w1_codes_%d" % g) for g in range(2)]
        w1_scales = [held([P, H], U8, "w1_scales_%d" % g) for g in range(2)]
        w1_bf = [held([P, PACK * H], BF16, "w1_bf%d" % g) for g in range(2)]

        def round_w1(g):
            dealt = w1_bf[g][:].rearrange("p (t m e j) -> p m j e t", t=PACK, e=2, j=PACK)
            by_channel = w1_raw[g][:].rearrange("p (j m e t) -> p m j e t", t=PACK, e=2, j=PACK)
            m = W1_SCALAR[g]
            nc.scalar.copy(dealt[:, :m], by_channel[:, :m])
            nc.vector.tensor_copy(out=dealt[:, m:], in_=by_channel[:, m:])

        def round_last():
            dealt = w1_bf[1][:].rearrange("p (t m e j) -> p m j e t", t=PACK, e=2, j=PACK)
            by_channel = w1_raw[1][:].rearrange("p (j m e t) -> p m j e t", t=PACK, e=2, j=PACK)
            m = W1_SCALAR[1]
            nc.vector.tensor_copy(out=dealt[:, :, :, :, :2], in_=by_channel[:, :, :, :, :2])
            nc.scalar.copy(dealt[:, :m, :, :, 2:], by_channel[:, :m, :, :, 2:])
            nc.vector.tensor_copy(out=dealt[:, m:, :, :, 2:], in_=by_channel[:, m:, :, :, 2:])

        def quantize_w1(g, t0, t1):
            cols = slice(t0 * P, t1 * P)
            nc.vector.quantize_mx(
                out=w1_codes[g][:, cols].bitcast(FP8X4),
                scales=w1_scales[g][:, cols],
                in_=w1_bf[g][:, t0 * P * PACK : t1 * P * PACK],
            )

        for j in range(PACK):
            for d in range(PIECES):
                gather(0, j, d, 0, V, d == 0)
        woven0 = held([P, BANKS * BAND], BF16, "woven0")
        weave(0, 0, BANKS, woven0[:])
        quantize_x(0, 0, BANKS, woven0[:])
        for j in range(PACK - 1):
            for a in range(2):
                for d in range(PIECES):
                    gather(1, j, d, a * half_v, (a + 1) * half_v, (j, a, d) not in ((1, 0, 1), (1, 1, 1), (2, 0, 1)))
        last = PACK - 1
        ahead = held([P, 4 * BAND], BF16, "woven_ahead")
        weave(1, 0, 4, ahead[:], False, 0, last)
        gather(1, last, 0, 0, 128, True)
        gather(1, last, 1, 0, 128, False)
        gather(1, last, 0, 128, 256, True)
        gather(1, last, 1, 128, 256, False)
        gather(1, last, 0, 256, 512, True)
        gather(1, last, 1, 256, 512, True)
        woven1 = [
            placed([P, 2 * BAND], BF16, "woven1_4", 0),
            placed([P, 2 * BAND], BF16, "woven1_6", 8192),
        ]
        weave(1, 0, 2, ahead[:, : 2 * BAND], False, last, PACK)
        weave(1, 2, 4, ahead[:, 2 * BAND :], False, last, PACK)
        quantize_x(1, 0, 2, ahead[:, : 2 * BAND])
        quantize_x(1, 2, 4, ahead[:, 2 * BAND :])
        round_w1(0)
        weave(1, 4, 5, woven1[0][:, :BAND])
        weave(1, 5, 6, woven1[0][:, BAND:], True)
        quantize_w1(0, 0, 2)
        quantize_w1(0, 2, PACK)
        round_last()
        quantize_w1(1, 0, 2)
        quantize_w1(1, 2, PACK)
        weave(1, 6, 7, woven1[1][:, :BAND], True)
        quantize_x(1, 4, 6, woven1[0][:], 8192 + 4096)
        weave(1, 7, 8, woven1[1][:, BAND:])
        quantize_x(1, 6, 8, woven1[1][:])

        unread = psum.tile([P, 2 * P], F32, name="unread", tag="bank%d" % (BANKS - 1))
        for n in range(WARM_PASSES):
            nc.tensor.matmul_mx(
                out=unread[:],
                lhsT=x_mx[1, 2][0].bitcast(FP8X4),
                lhsT_scale=x_mx[1, 2][1],
                rhs=x_mx[1, 2, 4][0][:].bitcast(FP8X4),
                rhs_scale=x_mx[1, 2, 4][1][:],
                start=True,
                stop=True,
            )

        banks = [psum.tile([P, PACK, P], F32, name="h_bank_%d" % b, tag="bank%d" % b) for b in range(BANKS)]

        def first_pass(g, b, t, start, stop):
            m_cols = slice(t * P, (t + 1) * P)
            nc.tensor.matmul_mx(
                out=banks[b][:, t, :],
                lhsT=w1_codes[g][:, m_cols].bitcast(FP8X4),
                lhsT_scale=w1_scales[g][:, m_cols],
                rhs=x_mx[g, b][0].bitcast(FP8X4),
                rhs_scale=x_mx[g, b][1],
                start=start,
                stop=stop,
            )

        for b in range(EARLY_BANKS):
            for t in range(PACK):
                first_pass(0, b, t, t == 0, False)

        h = [held([P, BAND], F32, "h_%d" % b) for b in range(BANKS)]

        def gelu(b, c0, c1):
            nc.scalar.activation(
                h[b][:, c0 * PACK : c1 * PACK].rearrange("p (v t) -> p v t", t=PACK),
                banks[b][:, :, c0:c1].rearrange("p t v -> p v t"),
                ACT.Gelu_apprx_tanh,
            )

        for b in range(BANKS):
            for t in range(PACK):
                if b < EARLY_BANKS:
                    first_pass(1, b, t, False, t == PACK - 1)
                else:
                    first_pass(1, b, t, True, False)
                    first_pass(0, b, t, False, True)
            if b < 2:
                for c0, c1 in FIRST_CUTS:
                    gelu(b, c0, c1)
            else:
                gelu(b, 0, P)

        slices = V // SLICE
        bands = [held([P, 2 * BAND], BF16, "bands_%d" % s) for s in range(slices)]

        def band(b, i, c0=0, c1=P):
            at = i * BAND + (b % 2) * (BAND // 2)
            dst = bands[b // 2][:, at + c0 * 2 : at + c1 * 2].rearrange("p (c x) -> p c x", x=RUN * PACK)
            src = h[b][:, c0 * PACK : c1 * PACK].rearrange("p (c d x) -> p d c x", d=PIECES, x=RUN * PACK)
            nc.vector.tensor_tensor(dst, src[:, 0], src[:, 1], ALU.add if i == 0 else ALU.subtract)

        def band_pass(acc, mt, i, codes, scales):
            nc.tensor.matmul_mx(
                out=acc,
                lhsT=w23_words[i][:, 2 * P * mt : 2 * P * (mt + 1)].bitcast(FP4X4),
                lhsT_scale=w23_scales[i][:, P * mt : P * (mt + 1)],
                rhs=codes.bitcast(FP8X4),
                rhs_scale=scales,
                start=(i == 0),
                stop=(i == 1),
            )

        def product(s, acc):
            codes = held([P, 2 * SLICE], U32, "band_codes_%d" % s)
            scales = held([P, 2 * SLICE], U8, "band_scales_%d" % s)
            nc.vector.quantize_mx(out=codes[:].bitcast(FP8X4), scales=scales[:], in_=bands[s][:])
            for mt in range(N // P):
                for i in range(2):
                    cols = slice(i * SLICE, (i + 1) * SLICE)
                    band_pass(acc[:, mt, :], mt, i, codes[:, cols], scales[:, cols])

        def store(acc, s0, s1):
            result = held([P, 2, (s1 - s0) * SLICE], F32, "result_%d" % s0)
            nc.scalar.activation(result[:], acc, ACT.Copy, scale=0.5)
            nc.sync.dma_start(
                out=out[:, s0 * SLICE : s1 * SLICE].rearrange("(mt p) v -> p mt v", p=P), in_=result[:]
            )

        def finish_last(s):
            accs = [psum.tile([P, SLICE], F32, name="acc_last_%d" % mt, tag="bank%d" % mt) for mt in range(N // P)]
            for i in range(2):
                codes = held([P, SLICE], U32, "last_codes_%d" % i)
                scales = held([P, SLICE], U8, "last_scales_%d" % i)
                nc.vector.quantize_mx(
                    out=codes[:].bitcast(FP8X4), scales=scales[:], in_=bands[s][:, i * BAND : (i + 1) * BAND]
                )
                for mt in range(N // P):
                    band_pass(accs[mt][:], mt, i, codes[:], scales[:])
            cols = slice(s * SLICE, (s + 1) * SLICE)
            results = [held([P, SLICE], F32, "result_last_%d" % mt) for mt in range(N // P)]
            nc.vector.tensor_scalar_mul(results[0][:], accs[0][:], 0.5)
            nc.sync.dma_start(out=out[:P, cols], in_=results[0][:])
            nc.scalar.activation(results[1][:], accs[1][:], ACT.Copy, scale=0.5)
            nc.scalar.dma_start(out=out[P:, cols], in_=results[1][:])

        acc01 = psum.tile([P, 2, 2 * SLICE], F32, name="acc01", tag="bank7")
        acc2 = psum.tile([P, 2, SLICE], F32, name="acc2", tag="bank6")
        for b in range(2):
            for c0, c1 in FIRST_CUTS:
                for i in range(2):
                    band(b, i, c0, c1)
        for b in range(2, BANKS):
            band(b, 0)
            if b == 2:
                product(0, acc01[:, :, :SLICE])
            if b == 4:
                product(1, acc01[:, :, SLICE:])
                store(acc01[:], 0, 2)
            if b == 6:
                product(2, acc2[:])
                store(acc2[:], 2, 3)
            band(b, 1)
        finish_last(slices - 1)
